import numpy as np, ml_dtypes
CORES = [25,29,65,69,153,157,193,197]
N = 8
import mx_ref
BF = ml_dtypes.bfloat16
def gcols(t, e):
    v = np.concatenate([t.reshape(8, 16, -1, 4), np.zeros((8, 16, 1, 4), BF)], axis=2)
    return np.ascontiguousarray(np.stack([v[g][:, e[g]] for g in range(8)])).reshape(128, -1)
def tile(rs):
    return np.stack(rs, axis=2).reshape(128, -1).astype(BF)
def pick(q, e):
    c = np.concatenate([q[0].reshape(128, -1, 4), np.zeros((128, 1, 4), np.uint8)], axis=1); s = np.concatenate([q[1], np.ones((16, 1), np.uint8)], axis=1)
    return (np.ascontiguousarray(c[:, e].reshape(128, -1)), np.ascontiguousarray(s[:, e]))
def join(*qs):
    return (np.concatenate([q[0] for q in qs], axis=1), np.concatenate([q[1] for q in qs], axis=1))
def put(q, e, v):
    c, s = q[0].reshape(128, -1, 4).copy(), q[1].copy(); c[:, e] = v[0].reshape(128, -1, 4); s[:, e] = v[1]
    return (c.reshape(128, -1), s)
def pk(c, s):
    return (np.ascontiguousarray(c), mx_ref.live(s))
def emit(q):
    return q[0], q[1]
def packed(v, rng):
    q = [mx_ref.quantize(np.ascontiguousarray(v[r])) for r in range(N)]
    return np.stack([a for a, b in q]), np.stack([mx_ref.plane(b, rng) for a, b in q])
def f(rng, *shape):
    return mx_ref.flush((rng.standard_normal(shape, dtype=np.float32) * np.exp2(rng.integers(-2, 3, shape[:-1] + (1,)))).astype(BF))
def wide(rng, *shape, cols=0):
    v = rng.standard_normal(shape, dtype=np.float32) * np.exp2(rng.integers(-12, 13, shape)).astype(np.float32)
    if cols: v *= np.repeat(np.exp2(rng.integers(-cols, cols + 1, shape[:-2] + (1, shape[-1] // 4))) * (rng.random(shape[:-2] + (1, shape[-1] // 4)) > 0.0625), 4, axis=-1).astype(np.float32)
    return mx_ref.flush(v.astype(BF))
C, K, R = 384, 96, 4
def lowest(p):
    return np.argsort(p[::16] + np.float32(0.0), axis=1, kind="stable")[:, :K]
def gput(t, e, s):
    o, w = t.reshape(8, 16, -1, 4).copy(), s.reshape(8, 16, -1, 4)
    for g in range(8): o[g][:, e[g]] = w[g]
    return o.reshape(128, -1)
def numbers_of(rng):
    return {"x": np.array(f(rng, N, 128, 4 * C)), "a": np.array(f(rng, N, 128, 4 * K)), "u": np.array(f(rng, N, 128, 512)), "v": np.array(f(rng, N, 128, 512))}
def weights(rng, w):
    c, p = packed(w, rng)
    return {"wc": c, "ws": p}
def still(rng):
    w = np.zeros((N, 128, 4, 128, 4), np.float32)
    i = np.arange(128)
    for b in range(4): w[:, i, b, i, b] = 32
    return weights(rng, w.reshape(N, 128, 2048).astype(BF))
def signs(rng):
    return np.stack([rng.permutation(8) % 2 * 2.0 - 1.0 for r in range(N)])
def digits(rng, t, s):
    x = t.astype(np.float32).reshape(N, 8, 16, -1, 4)
    b = ((s[..., None] >> np.arange(8)) & 1) * np.exp2(np.arange(8) - 23.0)
    x[:, :, 0] = 0
    x[:, :, 0, :, 0] = 1
    x[:, :, 8] = b[..., :4]
    x[:, :, 9] = b[..., 4:]
    z = x[:, :, 10:].shape
    x[:, :, 10:] = rng.integers(4, 8, z) * rng.choice([-1.0, 1.0], z) * 2.0 ** -20
    return x.reshape(t.shape).astype(BF)
def setup_inputs(rng):
    return {**numbers_of(rng), **weights(rng, f(rng, N, 128, 2048))}
def setup_inputs_ties(rng):
    d = numbers_of(rng)
    e = rng.permutation(N)
    for n in ("x", "a"):
        x = d[n].reshape(N, 8, 16, -1, 4)
        for r in range(N):
            k = rng.permutation(x.shape[3]) % 3
            if n == "x" and r == e[0]: k = np.zeros(C, int)
            p = x[r][:, :8, :3].copy()
            p[:, :, 2] = 0
            x[r][:, :8] = p[:, :, k]
        if n == "x": x[e[1]] = 0
        d[n] = x.reshape(N, 128, -1)
    u = d["u"].reshape(N, 8, 16, 128, 4)
    u[:, :, 8:, ::16] = 0
    w = np.array(f(rng, N, 128, 2048)).reshape(N, 8, 16, 4, 8, 16, 4)
    w[:, :, 8:, :, :, :8] = 0
    return {"x": d["x"], "a": d["a"], "u": u.reshape(N, 128, 512), "v": d["v"], **weights(rng, w.reshape(N, 128, 2048))}
def setup_inputs_near(rng):
    d = numbers_of(rng)
    turn = (1.0 - 2.0 * (np.arange(N) % 2))[:, None]
    g = signs(rng)[:1] * turn
    h = rng.choice([-1.0, 1.0], 8)[None, :] * turn
    size = np.where(signs(rng) > 0, 1.0, 2.0 ** -28)
    shift = np.stack([2 + 2 * rng.permutation(C // 2 - K - 1)[:8] for r in range(N)])
    shift[np.arange(N), np.argmax(g, axis=1)] = 0
    q = (C - 1 - np.arange(C) - shift[:, :, None]) % C // 2
    k = K // 2 + (K - np.arange(K)) // 2 + np.zeros((N, 8, 1), int)
    up = h[:, :, None] > 0
    d["x"] = digits(rng, d["x"], np.where(up, q, C // 2 - 1 - q))
    d["a"] = digits(rng, d["a"], np.where(up, k, C // 2 - 1 - k))
    far = np.where(g > 0, np.argmax(q, axis=2), np.argmin(q, axis=2))
    x = d["x"].reshape(N, 8, 16, C, 4)
    x[np.arange(N)[:, None], np.arange(8)[None, :], 0, far, 0] = 4096
    g = (g * size).astype(np.float32).astype(BF)
    h = (h * size).astype(np.float32).astype(BF)
    u = d["u"].reshape(N, 128, 128, 4)
    u[:, :, ::16] = 0
    for i in range(8):
        u[:, 16 * i, 16 * i, 0] = g[:, i]
        u[:, 16 * i + 8:16 * i + 10, 16 * i] = h[:, i, None, None]
    return {"x": x.reshape(N, 128, 4 * C), "a": d["a"], "u": u.reshape(N, 128, 512), "v": d["v"], **still(rng)}
def setup_inputs_huge(rng):
    d = numbers_of(rng)
    both = rng.permutation(N) % 2 == 0
    k = np.stack([rng.permutation(C) % 2 for r in range(N)])
    k[~both] = -1
    x = 2.0 ** 30 * (0.6 + 0.4 * rng.random((N, 8, 16, C, 4)))
    x[:, :, :8] *= np.where(k == 1, 2.0 ** -6, 1.0)[:, None, None, :, None]
    x[:, :, 8:] *= np.where(k == 0, 2.0 ** -6, 1.0)[:, None, None, :, None]
    a = 2.0 ** 30 * (0.6 + 0.4 * rng.random((N, 128, 4 * K)))
    s = np.ones((N, 8, 16, 1, 1))
    s[both, :, 8:] = -1
    s = s * signs(rng)[:, None, None, :, None] * 2.0 ** 30 * (1 - 0.25 * rng.random((N, 8, 16, 8, 4)))
    u = d["u"].reshape(N, 8, 16, 128, 4)
    u[:, :, :, ::16] = s.astype(np.float32).astype(BF)
    return {"x": x.astype(np.float32).reshape(N, 128, 4 * C).astype(BF), "a": a.astype(np.float32).astype(BF), "u": u.reshape(N, 128, 512), "v": d["v"], **still(rng)}
def setup_inputs_spread(rng):
    d = setup_inputs(rng)
    d["x"] = wide(rng, N, 128, 4 * C, cols=6)
    d["a"] = wide(rng, N, 128, 4 * K, cols=6)
    return d
def check_inputs(d):
    b = []
    for k in ("x", "a", "u", "v"):
        z = np.abs(d[k].astype(np.float32))
        if not (np.isfinite(z).all() and ((z == 0) | (z >= 2.0 ** -30) & (z <= 2.0 ** 30)).all()): b.append("a value of " + k)
    top = np.max((d["wc"] & 127).reshape(N, 16, 8, -1, 4), axis=(2, 4))
    s = np.stack([mx_ref.live(p) for p in d["ws"]])
    if (top == 127).any(): b.append("a code of wc")
    if not ((top == 0) & (s == 1) | (top > 0) & (s >= 88) & (s <= 157)).all(): b.append("a scale of ws")
    return b
def reference(x, a, u, v, wc, ws):
    qu = [mx_ref.quantize(u[r]) for r in range(N)]
    lay = [pk(wc[r], ws[r]) for r in range(N)]
    now = [x[r] for r in range(N)]
    came = [mx_ref.quantize(a[r]) for r in range(N)]
    for t in range(R):
        o, gone = [], []
        for r in range(N):
            o.append(lowest(mx_ref.matmul(qu[r], mx_ref.quantize(now[r]))))
            gone.append(mx_ref.quantize(gcols(now[r], o[r])))
            e = tile([np.maximum(mx_ref.matmul(pick(lay[r], np.arange(128 * b, 128 * b + 128)), came[r]), np.float32(0.0)) * np.float32(0.03125) for b in range(4)])
            now[r] = gput(now[r], o[r], e)
        came = [gone[(r - 1) % N] for r in range(N)]
    y, ol = np.zeros((N, 128, C), np.float32), np.zeros((N, 8, K), np.float32)
    oc, osc = np.zeros((N, 128, 4 * C), np.uint8), np.zeros((N, 16, C), np.uint8)
    for r in range(N):
        q = mx_ref.quantize(now[r])
        y[r] = mx_ref.matmul(mx_ref.quantize(v[r]), q)
        ol[r] = o[r]
        oc[r], osc[r] = emit(q)
    return {"y": y, "ol": ol, "oc": oc, "osc": osc}

@@ -1,0 +1,328 @@
+from concourse.mybir import dt, AluOpType as Alu, ActivationFunctionType as Act
+
+C, K, R = 384, 96, 4
+NB = C // 16
+NV = 14
+NS = NB - NV
+H0 = 16 * NV
+H1 = H0 + 16 * (NS // 2)
+N1 = NV - 2
+PAD = 128 - K
+Q4, U8 = "float8_e4m3fn_x4", "uint8"
+
+SCRATCH = {
+    "xs": ("sbuf", [128, 4 * C], "bfloat16"),
+    "xc": ("sbuf", [128, 4 * C], "bfloat16"),
+    "xq": ("sbuf", [128, C], Q4), "xp": ("sbuf", [128, C], U8),
+    "ut": ("sbuf", [128, 512], "bfloat16"), "uq": ("sbuf", [128, 128], Q4), "up": ("sbuf", [128, 128], U8),
+    "gq": ("sbuf", [128, 128], Q4), "gp": ("sbuf", [128, 128], U8),
+    "vt": ("sbuf", [128, 512], "bfloat16"), "vq": ("sbuf", [128, 128], Q4), "vp": ("sbuf", [128, 128], U8),
+    "wq": ("sbuf", [128, 512], Q4), "wp": ("sbuf", [128, 512], U8),
+    "pt": ("sbuf", [128, 4 * (PAD + R * K)], "bfloat16"),
+    "pq": ("sbuf", [128, 128 * (R - 1)], Q4), "pp": ("sbuf", [128, 128 * (R - 1)], U8),
+    "hq": ("sbuf", [128, K * (R - 1)], Q4), "hp": ("sbuf", [128, K * (R - 1)], U8),
+    "lq": ("sbuf", [128, PAD + R * K], Q4), "lp": ("sbuf", [128, PAD + R * K], U8),
+    "et": ("sbuf", [128, 4 * K], "bfloat16"),
+    "i1": ("sbuf", [128, C], "int32"), "i2": ("sbuf", [128, C], "int32"),
+    "i3": ("sbuf", [128, K], "int32"), "i4": ("sbuf", [128, K], "int32"),
+    "i5": ("sbuf", [128, 8], "int32"), "i6": ("sbuf", [128, 1], "int32"),
+    "uoff": ("sbuf", [128, 8], "uint16"),
+    "own": ("sbuf", [128, C], "bfloat16"), "oth": ("sbuf", [128, C], "bfloat16"),
+    "j4": ("sbuf", [128, C], "float32"), "step": ("sbuf", [128, K], "float32"),
+    "c1": ("sbuf", [128, 1], "float32"), "col": ("sbuf", [128, 1], "float32"),
+    "rm": ("sbuf", [128, C], "float32"), "hold": ("sbuf", [128, C], "float32"),
+    "eq": ("sbuf", [128, C], "bfloat16"), "tie": ("sbuf", [128, C], "bfloat16"),
+    "cmp": ("sbuf", [128, NV * C], "bfloat16"), "cnt": ("sbuf", [128, NV * (C // 2)], "float16"),
+    "sgn": ("sbuf", [128, NS * C], "bfloat16"),
+    "f3": ("sbuf", [128, 3 * NS], "float32"), "w3": ("sbuf", [128, 3 * NS], "float32"), "r3": ("sbuf", [128, 3 * NS], "float32"),
+    "roff": ("sbuf", [128, NB], "uint16"), "order": ("sbuf", [128, C], "float32"),
+    "pick": ("sbuf", [128, K], "float32"), "off4": ("sbuf", [128, 4 * K // 16], "uint16"),
+    "olt": ("sbuf", [128, K], "float32"), "yt": ("sbuf", [128, C], "float32"),
+    "pv": ("psum", [128, 512], "float32"), "ps": ("psum", [128, 512], "float32"),
+    "pw": ("psum", [128, 4 * 512], "float32"),
+}
+SEMAPHORES = ["lx", "lu", "la", "lw", "lv", "xc", "io1", "io2", "io3", "io4", "k1", "k2", "k3", "k4", "k5", "kown", "koth",
+              "qu", "gu", "qa", "qv", "qx", "qx2", "qp", "mmv", "mms", "mmw", "rm0", "rm1", "rm2", "h0", "h1", "h2", "eq", "tie",
+              "f3", "ca", "cb", "cc", "sc", "sd", "r3", "rof1", "roff", "order", "pick", "off4", "xs", "p1a", "p1b", "acc",
+              "relu", "pg", "olt", "ya", "yb", "outa", "outb", "sent", "ar1", "ar2", "ar3", "hop1", "hop2", "hop3"]
+
+
+def mask_of(engines):
+    m = 0
+    for e in engines:
+        m |= 1 << e
+    return m
+
+
+def way(T, topo, r):
+    src, dst = T.cores[r], T.cores[(r + 1) % len(T.cores)]
+    if topo.may_write(src, dst):
+        return dst, dst
+    via = [c for c in topo.cores_of(src) if T.rank_of(c) is None and topo.die(c) == topo.die(src) and topo.may_write(c, dst)]
+    return via[0], via[1]
+
+
+def first_leg(topo, src, a, b):
+    return topo.engines(src, a)[:8], topo.engines(src, b)[-4:]
+
+
+def landing(T, t):
+    lo = PAD + K * t
+    return T.lq[:, lo:lo + K].bitcast(dt.uint8), T.lp[:, lo:lo + K]
+
+
+def hand_on(g, core, T, topo):
+    n = len(T.cores)
+    for r in range(n):
+        a, b = way(T, topo, r)
+        if core not in (a, b):
+            continue
+        src, dst = T.cores[r], T.cores[(r + 1) % n]
+        ea, eb = first_leg(topo, src, a, b)
+        out = topo.engines(core, dst)
+        rid, pid = topo.addr(dst, core)
+        for t in range(1, R):
+            lo = K * (t - 1)
+            g.wait_ge(T.sem["hop%d" % t], len(ea) if core == a else len(eb))
+            held = T.hq[:, lo:lo + K].bitcast(dt.uint8) if core == a else T.hp[:, lo:lo + K]
+            g.remote_dma(landing(T, t)[0 if core == a else 1], held, T.sem["ar%d" % t], T.sem.sent, pid, rid, mask_of(out))
+        g.wait_ge(T.sem.sent, (R - 1) * len(out))
+
+
+def rank_program(g, core, T, topo):
+    rank = T.rank_of(core)
+    if rank is None:
+        hand_on(g, core, T, topo)
+        return
+    n = len(T.cores)
+    V, S, PE, SY = g.vector, g.scalar, g.tensor, g.sync
+    count = {}
+
+    def inc(ins, name, by=1):
+        ins.then_inc(T.sem[name], by)
+        count[name] = count.get(name, 0) + by
+
+    def wait(q, *names):
+        for name in names:
+            q.wait_ge(T.sem[name], count[name])
+
+    nxt = T.cores[(rank + 1) % n]
+    to_a, to_b = way(T, topo, rank)
+    ea, eb = first_leg(topo, core, to_a, to_b)
+    direct = to_a == nxt
+    prev = (rank - 1) % n
+    fa, fb = way(T, topo, prev)
+    if fa == core:
+        pa, pb = first_leg(topo, T.cores[prev], fa, fb)
+        arrive = len(pa) + len(pb)
+    else:
+        arrive = len(topo.engines(fa, core)) + len(topo.engines(fb, core))
+
+    inc(S.dma_start(T.xs[:], T.x[:]), "lx", 16)
+    inc(SY.dma_start(T.ut[:], T.u[:]), "lu", 16)
+    wait(SY, "lx")
+    inc(SY.dma_start(T.pt[:, 4 * PAD:4 * (PAD + K)], T.a[:]), "la", 16)
+    inc(SY.dma_start(T.wp[:], T.ws[:]), "lw", 16)
+    inc(SY.dma_start(T.wq[:].bitcast(dt.uint8), T.wc[:]), "lw", 16)
+    inc(SY.dma_start(T.xc[:], T.x[:]), "xc", 16)
+    inc(SY.dma_start(T.vt[:], T.v[:]), "lv", 16)
+
+    inc(g.iota(T.i5[:], [[16, 8]], 0, 0), "io1")
+    inc(g.iota(T.i1[:], [[0, NB], [-1, 16]], 16, 1), "io3")
+    inc(g.iota(T.i3[:], [[0, K // 4], [-4, 4]], 16, 1), "io2")
+    inc(g.iota(T.j4[:], [[4, C]], 0, 0, allow_small_or_imprecise_dtypes=True), "io4")
+    inc(V.memset(T.pt[:, 0:4 * PAD], 0.0), "k1")
+    inc(V.memset(T.f3[:], 0.0), "k1")
+    inc(V.memset(T.w3[:, 0:3 * NS:3], 0.0), "k1")
+    inc(V.memset(T.w3[:, 1:3 * NS:3], 1.0), "k1")
+    inc(V.memset(T.w3[:, 2:3 * NS:3], 0.5), "k1")
+    wait(V, "io1")
+    inc(V.tensor_copy(T.uoff[:], T.i5[:]), "k1")
+    wait(V, "io3")
+    inc(V.tensor_scalar(T.i2[:], T.i1[:], 15, None, Alu.bitwise_and), "k4")
+    wait(V, "io2")
+    inc(V.tensor_scalar(T.i4[:], T.i3[:], 12, None, Alu.bitwise_and), "k2")
+    inc(V.tensor_scalar(T.i6[:], T.i3[:, 0:1], 3, None, Alu.bitwise_and), "k2")
+    wait(V, "k4")
+    inc(V.tensor_scalar(T.own[:], T.i2[:], 0.0, None, Alu.is_equal), "kown")
+    wait(S, "kown")
+    inc(S.activation(T.oth[:], T.own[:], Act.Identity, bias=1.0, scale=-1.0), "koth")
+    wait(V, "k2")
+    inc(V.tensor_scalar(T.step[:], T.i4[:], 0.0, -1.0e6, Alu.is_equal, Alu.mult), "k3")
+    inc(V.tensor_scalar(T.c1[:], T.i4[:, 0:1], 512.0, -6144.0, Alu.mult, Alu.add), "k3")
+
+    wait(V, "lu")
+    inc(V.quantize_mx(T.uq[:], T.up[:], T.ut[:]), "qu")
+    wait(V, "k3")
+    inc(V.tensor_scalar(T.step[:], T.step[:], 2048.0, None, Alu.add), "k5")
+    inc(V.tensor_tensor(T.col[:], T.c1[:], T.i6[:], Alu.add), "k5")
+    wait(V, "k1", "qu")
+    inc(V.tensor_copy(T.gq[:].bitcast(dt.uint32), T.uq[:].bitcast(dt.uint32).indirect(T.uoff[:])), "gu")
+    inc(V.tensor_copy(T.gp[:], T.up[:].indirect(T.uoff[:])), "gu")
+    wait(PE, "gu")
+
+    half = C // 2
+    for t in range(R):
+        last = t == R - 1
+        wait(V, "lx" if t == 0 else "xs")
+        inc(V.quantize_mx(T.xq[:], T.xp[:], T.xs[:]), "qx")
+        lo = K * t
+        if t > 0:
+            wait(V, "pg")
+            o = 128 * (t - 1)
+            inc(V.quantize_mx(T.pq[:, o:o + 128], T.pp[:, o:o + 128], T.pt[:, 4 * lo:4 * lo + 512]), "qp")
+            wait(g, "qp")
+            h = K * (t - 1)
+            da, db = landing(T, t) if direct else (T.hq[:, h:h + K].bitcast(dt.uint8), T.hp[:, h:h + K])
+            sem = T.sem[("ar%d" if direct else "hop%d") % t]
+            rid, pid = topo.addr(to_a, core)
+            g.remote_dma(da, T.pq[:, o + PAD:o + 128].bitcast(dt.uint8), sem, T.sem.sent, pid, rid, mask_of(ea))
+            rid, pid = topo.addr(to_b, core)
+            g.remote_dma(db, T.pp[:, o + PAD:o + 128], sem, T.sem.sent, pid, rid, mask_of(eb))
+        if t == 2:
+            wait(V, "lv")
+            inc(V.quantize_mx(T.vq[:], T.vp[:], T.vt[:]), "qv")
+
+        wait(PE, "qx")
+        inc(PE.matmul_mx(T.pv[:, 0:C], T.gq[:], T.gp[:], T.xq[:], T.xp[:], True, True), "mmv")
+        inc(PE.matmul_mx(T.ps[:, 0:C], T.gq[:], T.gp[:], T.xq[:], T.xp[:], True, True), "mms")
+
+        wait(V, "mmv")
+        if t == 0:
+            wait(V, "kown", "koth")
+        inc(V.tensor_tensor(T.rm[:, H0:H1], T.pv[:, H0:H1], T.own[:, H0:H1], Alu.mult), "rm0")
+        inc(V.tensor_tensor(T.rm[:, H1:C], T.pv[:, H1:C], T.own[:, H1:C], Alu.mult), "rm1")
+        wait(V, "rm0")
+        inc(V.tensor_tensor_scan(T.hold[:, H0:H1], T.oth[:, H0:H1], T.rm[:, H0:H1], 0.0, Alu.mult, Alu.add), "h0")
+        inc(V.tensor_tensor(T.rm[:, 0:H0], T.pv[:, 0:H0], T.own[:, 0:H0], Alu.mult), "rm2")
+        wait(V, "rm1")
+        inc(V.tensor_tensor_scan(T.hold[:, H1:C], T.oth[:, H1:C], T.rm[:, H1:C], 0.0, Alu.mult, Alu.add), "h1")
+        wait(V, "rm2")
+        inc(V.tensor_tensor_scan(T.hold[:, 0:H0], T.oth[:, 0:H0], T.rm[:, 0:H0], 0.0, Alu.mult, Alu.add), "h2")
+        wait(V, "h0", "h1")
+        inc(V.tensor_tensor(T.eq[:, H0:C], T.pv[:, H0:C], T.hold[:, H0:C], Alu.is_equal), "eq")
+        wait(V, "h2")
+        inc(V.tensor_tensor(T.eq[:, 0:H0], T.pv[:, 0:H0], T.hold[:, 0:H0], Alu.is_equal), "eq")
+
+        wait(S, "mms", "h0")
+        for i in range(NS):
+            if 16 * (NV + i) == H1:
+                wait(S, "h1")
+            e = 16 * (NV + i) + 16
+            inc(S.activation(T.sgn[:, C * i:C * i + C], T.ps[:, 0:C], Act.Sign, bias=T.hold[:, e - 1:e], scale=-1.0),
+                "p1a" if i < NS - 1 else "p1b")
+        for i in range(NS):
+            if i == 0:
+                wait(S, "p1a")
+            if i == NS - 1:
+                wait(S, "p1b")
+            e = 16 * (NV + i) + 16
+            v = T.sgn[:, C * i:C * i + e]
+            inc(S.activation(v, v, Act.Sign, bias=0.5, accum_out=T.f3[:, 3 * i:3 * i + 1]), "acc")
+            if e < C:
+                v = T.sgn[:, C * i + e:C * i + C]
+                inc(S.activation(v, v, Act.Sign, bias=-0.5, accum_out=T.f3[:, 3 * i + 1:3 * i + 2]), "acc")
+
+        def compare(c, name):
+            e = 16 * c + 16
+            s = T.hold[:, e - 1:e]
+            inc(V.tensor_scalar(T.cmp[:, C * c:C * c + e], T.pv[:, 0:e], s, None, Alu.is_le), name)
+            inc(V.tensor_scalar(T.cmp[:, C * c + e:C * c + C], T.pv[:, e:C], s, None, Alu.is_lt), name)
+
+        def add_up(c, name):
+            inc(V.tensor_tensor_scan(T.cnt[:, half * c:half * c + half], T.cmp[:, C * c:C * c + half], T.cmp[:, C * c + half:C * c + C],
+                                     T.tie[:, 16 * c + 15:16 * c + 16], Alu.add, Alu.add), name)
+
+        for c in range(N1):
+            compare(c, "ca")
+            if c == 0:
+                wait(V, "eq")
+                inc(V.tensor_tensor_scan(T.tie[:], T.oth[:], T.eq[:], 0.0, Alu.mult, Alu.subtract), "tie")
+            if c == 1:
+                wait(V, "tie")
+                inc(V.tensor_scalar(T.f3[:, 2:3 * NS:3], T.tie[:, H0 + 15:C:16], float(half), None, Alu.add), "f3")
+            if c == 6 and t == 0:
+                wait(V, "la")
+                inc(V.quantize_mx(T.lq[:, 0:128], T.lp[:, 0:128], T.pt[:, 0:512]), "qa")
+
+        if t == 0:
+            wait(PE, "qa", "lw")
+        else:
+            PE.wait_ge(T.sem["ar%d" % t], arrive)
+        for b in range(4):
+            inc(PE.matmul_mx(T.pw[:, 512 * b:512 * b + 128], T.wq[:, 128 * b:128 * b + 128], T.wp[:, 128 * b:128 * b + 128],
+                             T.lq[:, lo:lo + 128], T.lp[:, lo:lo + 128], True, True), "mmw")
+        wait(S, "mmw")
+        for b in range(4):
+            inc(S.activation(T.et[:, b:4 * K:4], T.pw[:, 512 * b + PAD:512 * b + 128], Act.Relu, scale=0.03125), "relu")
+
+        compare(N1, "cb")
+        wait(V, "ca")
+        for c in range(N1):
+            add_up(c, "sc")
+        compare(N1 + 1, "cc")
+        wait(V, "sc")
+        inc(V.tensor_copy(T.roff[:, 0:N1], T.cnt[:, half - 1:half * N1:half]), "rof1")
+        wait(V, "cb")
+        add_up(N1, "sd")
+        wait(V, "cc")
+        add_up(N1 + 1, "sd")
+        wait(V, "rof1")
+        if t == 0:
+            wait(V, "io4", "k5")
+        inc(V.tensor_copy(T.order[:].indirect(T.roff[:, 0:N1]), T.j4[:, 0:16 * N1]), "order")
+        wait(V, "f3", "acc")
+        inc(V.tensor_tensor_scan(T.r3[:], T.w3[:], T.f3[:], 0.0, Alu.mult, Alu.add), "r3")
+        wait(V, "sd")
+        inc(V.tensor_copy(T.roff[:, N1:NV], T.cnt[:, half * N1 + half - 1:half * NV:half]), "roff")
+        wait(V, "r3")
+        inc(V.tensor_copy(T.roff[:, NV:NB], T.r3[:, 2:3 * NS:3]), "roff")
+        wait(V, "roff", "order")
+        inc(V.tensor_copy(T.order[:].indirect(T.roff[:, N1:NB]), T.j4[:, 16 * N1:C]), "order")
+
+        wait(V, "order")
+        inc(V.tensor_tensor_scan(T.pick[:], T.step[:], T.order[:, 0:K], 0.0, Alu.add, Alu.max), "pick")
+        wait(V, "pick")
+        inc(V.tensor_scalar(T.off4[:], T.pick[:, 3:K:4], T.col[:], None, Alu.add), "off4")
+        wait(V, "off4", "relu")
+        if 0 < t < R - 1:
+            wait(V, "xc")
+        inc(V.tensor_copy(T.xs[:].indirect(T.off4[:]), T.et[:]), "xs")
+
+        if not last:
+            wait(S, "off4", "xc")
+            p0 = 4 * (PAD + K * (t + 1))
+            inc(S.activation(T.pt[:, p0:p0 + 4 * K], T.xc[:].indirect(T.off4[:]), Act.Copy), "pg")
+            if t < R - 2:
+                wait(SY, "xs", "pg")
+                inc(SY.dma_start(T.xc[:], T.xs[:]), "xc", 16)
+        else:
+            wait(S, "order")
+            inc(S.activation(T.olt[:], T.order[:, 0:K], Act.Identity, scale=0.25), "olt")
+            wait(SY, "olt")
+            inc(SY.dma_start(T.ol[:], T.olt[0:128:16, :]), "outa", 16)
+
+    wait(V, "xs")
+    inc(V.quantize_mx(T.xq[:, 0:half], T.xp[:, 0:half], T.xs[:, 0:4 * half]), "qx")
+    inc(V.quantize_mx(T.xq[:, half:C], T.xp[:, half:C], T.xs[:, 4 * half:4 * C]), "qx2")
+    wait(PE, "qv", "qx")
+    inc(PE.matmul_mx(T.ps[:, 0:half], T.vq[:], T.vp[:], T.xq[:, 0:half], T.xp[:, 0:half], True, True), "mms")
+    wait(PE, "qx2")
+    inc(PE.matmul_mx(T.pv[:, 0:half], T.vq[:], T.vp[:], T.xq[:, half:C], T.xp[:, half:C], True, True), "mmv")
+    wait(S, "mms")
+    inc(S.activation(T.yt[:, 0:half], T.ps[:, 0:half], Act.Copy), "ya")
+    wait(V, "mmv")
+    inc(V.tensor_copy(T.yt[:, half:C], T.pv[:, 0:half]), "yb")
+    wait(SY, "qx", "qx2")
+    inc(SY.dma_start(T.oc[:], T.xq[:].bitcast(dt.uint8)), "outa", 16)
+    for k in range(2):
+        inc(SY.dma_start(T.osc[4 * k:4 * k + 4, :], T.xp[32 * k:32 * k + 4, :]), "outa", 16)
+    wait(S, "ya", "qx2")
+    inc(S.dma_start(T.y[:, 0:half], T.yt[:, 0:half]), "outb", 16)
+    for k in range(2, 4):
+        inc(S.dma_start(T.osc[4 * k:4 * k + 4, :], T.xp[32 * k:32 * k + 4, :]), "outb", 16)
+    wait(SY, "yb")
+    inc(SY.dma_start(T.y[:, half:C], T.yt[:, half:C]), "outa", 16)
+    wait(SY, "outa")
+    wait(S, "outb")
+    g.wait_ge(T.sem.sent, (R - 1) * (len(ea) + len(eb)))

@@ -5,9 +5,10 @@ NB = C // 16
 NV = 14
 NS = NB - NV
 H0 = 16 * NV
-H1 = H0 + 16 * (NS // 2)
 N1 = NV - 2
 PAD = 128 - K
+ROW = C + 2
+UP, TINY = 1.25 * 2.0 ** -24, 2.0 ** -124
 Q4, U8 = "float8_e4m3fn_x4", "uint8"
 
 SCRATCH = {
@@ -33,17 +34,17 @@ SCRATCH = {
     "rm": ("sbuf", [128, C], "float32"), "hold": ("sbuf", [128, C], "float32"),
     "eq": ("sbuf", [128, C], "bfloat16"), "tie": ("sbuf", [128, C], "bfloat16"),
     "cmp": ("sbuf", [128, NV * C], "bfloat16"), "cnt": ("sbuf", [128, NV * (C // 2)], "float16"),
-    "sgn": ("sbuf", [128, NS * C], "bfloat16"),
-    "f3": ("sbuf", [128, 3 * NS], "float32"), "w3": ("sbuf", [128, 3 * NS], "float32"), "r3": ("sbuf", [128, 3 * NS], "float32"),
+    "sgn": ("sbuf", [128, NS * ROW], "bfloat16"),
+    "ab": ("sbuf", [128, NS], "float32"), "sup": ("sbuf", [128, NS], "float32"), "acc": ("sbuf", [128, NS], "float32"),
     "roff": ("sbuf", [128, NB], "uint16"), "order": ("sbuf", [128, C], "float32"),
     "pick": ("sbuf", [128, K], "float32"), "off4": ("sbuf", [128, 4 * K // 16], "uint16"),
     "olt": ("sbuf", [128, K], "float32"), "yt": ("sbuf", [128, C], "float32"),
-    "pv": ("psum", [128, 512], "float32"), "ps": ("psum", [128, 512], "float32"),
+    "ph": ("psum", [128, 512], "float32"), "pv": ("psum", [128, 512], "float32"), "ps": ("psum", [128, 512], "float32"),
     "pw": ("psum", [128, 4 * 512], "float32"),
 }
-SEMAPHORES = ["lx", "lu", "la", "lw", "lv", "xc", "io1", "io2", "io3", "io4", "k1", "k2", "k3", "k4", "k5", "kown", "koth",
-              "qu", "gu", "qa", "qv", "qx", "qx2", "qp", "mmv", "mms", "mmw", "rm0", "rm1", "rm2", "h0", "h1", "h2", "eq", "tie",
-              "f3", "ca", "cb", "cc", "sc", "sd", "r3", "rof1", "roff", "order", "pick", "off4", "xs", "p1a", "p1b", "acc",
+SEMAPHORES = ["lx", "lx2", "lu", "la", "lw", "lv", "xc", "io1", "io2", "io3", "io4", "k1", "k2", "k3", "k4", "k5", "kown", "koth",
+              "qu", "gu", "qa", "qv", "qx", "qx2", "qp", "mmh", "mmv", "mms", "mmw", "rm1", "rm2", "h1", "h2", "eq", "tie",
+              "ab", "sup", "f3", "ca", "cb", "cc", "sc", "sd", "rof1", "roff", "order", "pick", "off4", "xs", "p1a", "p1b", "acc",
               "relu", "pg", "olt", "ya", "yb", "outa", "outb", "sent", "ar1", "ar2", "ar3", "hop1", "hop2", "hop3"]
 
 
@@ -118,9 +119,10 @@ def rank_program(g, core, T, topo):
     else:
         arrive = len(topo.engines(fa, core)) + len(topo.engines(fb, core))
 
-    inc(S.dma_start(T.xs[:], T.x[:]), "lx", 16)
+    inc(S.dma_start(T.xs[:, 4 * H0:4 * C], T.x[:, 4 * H0:4 * C]), "lx", 16)
     inc(SY.dma_start(T.ut[:], T.u[:]), "lu", 16)
-    wait(SY, "lx")
+    inc(S.dma_start(T.xs[:, 0:4 * H0], T.x[:, 0:4 * H0]), "lx2", 16)
+    wait(SY, "lx2")
     inc(SY.dma_start(T.pt[:, 4 * PAD:4 * (PAD + K)], T.a[:]), "la", 16)
     inc(SY.dma_start(T.wp[:], T.ws[:]), "lw", 16)
     inc(SY.dma_start(T.wq[:].bitcast(dt.uint8), T.wc[:]), "lw", 16)
@@ -132,10 +134,6 @@ def rank_program(g, core, T, topo):
     inc(g.iota(T.i3[:], [[0, K // 4], [-4, 4]], 16, 1), "io2")
     inc(g.iota(T.j4[:], [[4, C]], 0, 0, allow_small_or_imprecise_dtypes=True), "io4")
     inc(V.memset(T.pt[:, 0:4 * PAD], 0.0), "k1")
-    inc(V.memset(T.f3[:], 0.0), "k1")
-    inc(V.memset(T.w3[:, 0:3 * NS:3], 0.0), "k1")
-    inc(V.memset(T.w3[:, 1:3 * NS:3], 1.0), "k1")
-    inc(V.memset(T.w3[:, 2:3 * NS:3], 0.5), "k1")
     wait(V, "io1")
     inc(V.tensor_copy(T.uoff[:], T.i5[:]), "k1")
     wait(V, "io3")
@@ -147,27 +145,32 @@ def rank_program(g, core, T, topo):
     inc(V.tensor_scalar(T.own[:], T.i2[:], 0.0, None, Alu.is_equal), "kown")
     wait(S, "kown")
     inc(S.activation(T.oth[:], T.own[:], Act.Identity, bias=1.0, scale=-1.0), "koth")
-    wait(V, "k2")
-    inc(V.tensor_scalar(T.step[:], T.i4[:], 0.0, -1.0e6, Alu.is_equal, Alu.mult), "k3")
-    inc(V.tensor_scalar(T.c1[:], T.i4[:, 0:1], 512.0, -6144.0, Alu.mult, Alu.add), "k3")
 
     wait(V, "lu")
     inc(V.quantize_mx(T.uq[:], T.up[:], T.ut[:]), "qu")
-    wait(V, "k3")
-    inc(V.tensor_scalar(T.step[:], T.step[:], 2048.0, None, Alu.add), "k5")
-    inc(V.tensor_tensor(T.col[:], T.c1[:], T.i6[:], Alu.add), "k5")
+    wait(V, "k2")
+    inc(V.tensor_scalar(T.step[:], T.i4[:], 0.0, -1.0e6, Alu.is_equal, Alu.mult), "k3")
+    inc(V.tensor_scalar(T.c1[:], T.i4[:, 0:1], 512.0, -6144.0, Alu.mult, Alu.add), "k3")
     wait(V, "k1", "qu")
     inc(V.tensor_copy(T.gq[:].bitcast(dt.uint32), T.uq[:].bitcast(dt.uint32).indirect(T.uoff[:])), "gu")
     inc(V.tensor_copy(T.gp[:], T.up[:].indirect(T.uoff[:])), "gu")
     wait(PE, "gu")
 
     half = C // 2
+    NH = C - H0
     for t in range(R):
         last = t == R - 1
         wait(V, "lx" if t == 0 else "xs")
-        inc(V.quantize_mx(T.xq[:], T.xp[:], T.xs[:]), "qx")
+        inc(V.quantize_mx(T.xq[:, H0:C], T.xp[:, H0:C], T.xs[:, 4 * H0:4 * C]), "qx")
+        if t == 0:
+            wait(V, "lx2")
+        inc(V.quantize_mx(T.xq[:, 0:H0], T.xp[:, 0:H0], T.xs[:, 0:4 * H0]), "qx2")
         lo = K * t
-        if t > 0:
+        if t == 0:
+            wait(V, "k3")
+            inc(V.tensor_scalar(T.step[:], T.step[:], 2048.0, None, Alu.add), "k5")
+            inc(V.tensor_tensor(T.col[:], T.c1[:], T.i6[:], Alu.add), "k5")
+        else:
             wait(V, "pg")
             o = 128 * (t - 1)
             inc(V.quantize_mx(T.pq[:, o:o + 128], T.pp[:, o:o + 128], T.pt[:, 4 * lo:4 * lo + 512]), "qp")
@@ -179,49 +182,41 @@ def rank_program(g, core, T, topo):
             g.remote_dma(da, T.pq[:, o + PAD:o + 128].bitcast(dt.uint8), sem, T.sem.sent, pid, rid, mask_of(ea))
             rid, pid = topo.addr(to_b, core)
             g.remote_dma(db, T.pp[:, o + PAD:o + 128], sem, T.sem.sent, pid, rid, mask_of(eb))
-        if t == 2:
-            wait(V, "lv")
-            inc(V.quantize_mx(T.vq[:], T.vp[:], T.vt[:]), "qv")
 
         wait(PE, "qx")
+        inc(PE.matmul_mx(T.ph[:, 0:NH], T.gq[:], T.gp[:], T.xq[:, H0:C], T.xp[:, H0:C], True, True), "mmh")
+        wait(PE, "qx2")
         inc(PE.matmul_mx(T.pv[:, 0:C], T.gq[:], T.gp[:], T.xq[:], T.xp[:], True, True), "mmv")
         inc(PE.matmul_mx(T.ps[:, 0:C], T.gq[:], T.gp[:], T.xq[:], T.xp[:], True, True), "mms")
 
-        wait(V, "mmv")
+        wait(V, "mmh")
         if t == 0:
             wait(V, "kown", "koth")
-        inc(V.tensor_tensor(T.rm[:, H0:H1], T.pv[:, H0:H1], T.own[:, H0:H1], Alu.mult), "rm0")
-        inc(V.tensor_tensor(T.rm[:, H1:C], T.pv[:, H1:C], T.own[:, H1:C], Alu.mult), "rm1")
-        wait(V, "rm0")
-        inc(V.tensor_tensor_scan(T.hold[:, H0:H1], T.oth[:, H0:H1], T.rm[:, H0:H1], 0.0, Alu.mult, Alu.add), "h0")
+        inc(V.tensor_tensor(T.rm[:, H0:C], T.ph[:, 0:NH], T.own[:, H0:C], Alu.mult), "rm1")
+        wait(V, "mmv")
         inc(V.tensor_tensor(T.rm[:, 0:H0], T.pv[:, 0:H0], T.own[:, 0:H0], Alu.mult), "rm2")
         wait(V, "rm1")
-        inc(V.tensor_tensor_scan(T.hold[:, H1:C], T.oth[:, H1:C], T.rm[:, H1:C], 0.0, Alu.mult, Alu.add), "h1")
+        inc(V.tensor_tensor_scan(T.hold[:, H0:C], T.oth[:, H0:C], T.rm[:, H0:C], 0.0, Alu.mult, Alu.add), "h1")
         wait(V, "rm2")
         inc(V.tensor_tensor_scan(T.hold[:, 0:H0], T.oth[:, 0:H0], T.rm[:, 0:H0], 0.0, Alu.mult, Alu.add), "h2")
-        wait(V, "h0", "h1")
+        wait(V, "h1")
         inc(V.tensor_tensor(T.eq[:, H0:C], T.pv[:, H0:C], T.hold[:, H0:C], Alu.is_equal), "eq")
         wait(V, "h2")
         inc(V.tensor_tensor(T.eq[:, 0:H0], T.pv[:, 0:H0], T.hold[:, 0:H0], Alu.is_equal), "eq")
 
-        wait(S, "mms", "h0")
-        for i in range(NS):
-            if 16 * (NV + i) == H1:
-                wait(S, "h1")
+        wait(S, "h1")
+        inc(S.activation(T.ab[:], T.hold[:, H0 + 15:C:16], Act.Abs, bias=TINY, scale=UP), "ab")
+        wait(S, "mms")
+        for i in range(NS - 1):
             e = 16 * (NV + i) + 16
-            inc(S.activation(T.sgn[:, C * i:C * i + C], T.ps[:, 0:C], Act.Sign, bias=T.hold[:, e - 1:e], scale=-1.0),
+            inc(S.activation(T.sgn[:, ROW * i + e:ROW * i + C], T.ps[:, e:C], Act.Sign, bias=T.hold[:, e - 1:e], scale=-1.0), "p1a")
+        wait(V, "ab")
+        inc(V.tensor_tensor(T.sup[:], T.hold[:, H0 + 15:C:16], T.ab[:], Alu.add), "sup")
+        wait(S, "sup")
+        for i in range(NS):
+            e = 16 * (NV + i) + 16
+            inc(S.activation(T.sgn[:, ROW * i:ROW * i + e], T.ps[:, 0:e], Act.Sign, bias=T.sup[:, i:i + 1], scale=-1.0),
                 "p1a" if i < NS - 1 else "p1b")
-        for i in range(NS):
-            if i == 0:
-                wait(S, "p1a")
-            if i == NS - 1:
-                wait(S, "p1b")
-            e = 16 * (NV + i) + 16
-            v = T.sgn[:, C * i:C * i + e]
-            inc(S.activation(v, v, Act.Sign, bias=0.5, accum_out=T.f3[:, 3 * i:3 * i + 1]), "acc")
-            if e < C:
-                v = T.sgn[:, C * i + e:C * i + C]
-                inc(S.activation(v, v, Act.Sign, bias=-0.5, accum_out=T.f3[:, 3 * i + 1:3 * i + 2]), "acc")
 
         def compare(c, name):
             e = 16 * c + 16
@@ -240,10 +235,17 @@ def rank_program(g, core, T, topo):
                 inc(V.tensor_tensor_scan(T.tie[:], T.oth[:], T.eq[:], 0.0, Alu.mult, Alu.subtract), "tie")
             if c == 1:
                 wait(V, "tie")
-                inc(V.tensor_scalar(T.f3[:, 2:3 * NS:3], T.tie[:, H0 + 15:C:16], float(half), None, Alu.add), "f3")
+                inc(V.tensor_scalar(T.sgn[:, C:ROW * NS:ROW], T.tie[:, H0 + 15:C:16], 16.0, None, Alu.add), "f3")
             if c == 6 and t == 0:
                 wait(V, "la")
                 inc(V.quantize_mx(T.lq[:, 0:128], T.lp[:, 0:128], T.pt[:, 0:512]), "qa")
+
+        wait(S, "f3", "p1a")
+        for i in range(NS):
+            if i == NS - 1:
+                wait(S, "p1b")
+            v = T.sgn[:, ROW * i:ROW * i + C + 1]
+            inc(S.activation(v, v, Act.Relu, accum_out=T.acc[:, i:i + 1]), "acc")
 
         if t == 0:
             wait(PE, "qa", "lw")
@@ -271,17 +273,18 @@ def rank_program(g, core, T, topo):
         if t == 0:
             wait(V, "io4", "k5")
         inc(V.tensor_copy(T.order[:].indirect(T.roff[:, 0:N1]), T.j4[:, 0:16 * N1]), "order")
-        wait(V, "f3", "acc")
-        inc(V.tensor_tensor_scan(T.r3[:], T.w3[:], T.f3[:], 0.0, Alu.mult, Alu.add), "r3")
+        wait(V, "acc")
+        inc(V.tensor_scalar(T.roff[:, NV:NB], T.acc[:], -16.0, None, Alu.add), "roff")
         wait(V, "sd")
         inc(V.tensor_copy(T.roff[:, N1:NV], T.cnt[:, half * N1 + half - 1:half * NV:half]), "roff")
-        wait(V, "r3")
-        inc(V.tensor_copy(T.roff[:, NV:NB], T.r3[:, 2:3 * NS:3]), "roff")
         wait(V, "roff", "order")
         inc(V.tensor_copy(T.order[:].indirect(T.roff[:, N1:NB]), T.j4[:, 16 * N1:C]), "order")
 
         wait(V, "order")
         inc(V.tensor_tensor_scan(T.pick[:], T.step[:], T.order[:, 0:K], 0.0, Alu.add, Alu.max), "pick")
+        if t == 1:
+            wait(V, "lv")
+            inc(V.quantize_mx(T.vq[:], T.vp[:], T.vt[:]), "qv")
         wait(V, "pick")
         inc(V.tensor_scalar(T.off4[:], T.pick[:, 3:K:4], T.col[:], None, Alu.add), "off4")
         wait(V, "off4", "relu")

@@ -2,12 +2,18 @@ from concourse.mybir import dt, AluOpType as Alu, ActivationFunctionType as Act
 
 C, K, R = 384, 96, 4
 NB = C // 16
-NV = 14
-NS = NB - NV
-H0 = 16 * NV
-N1 = NV - 2
+TW = 128
+TB = TW // 16
+NS3 = 7
+H0 = 2 * TW
+HW = TW // 2
+HB = TB // 2
+HALF = C // 2
 PAD = 128 - K
-ROW = C + 2
+ROW = TW + 2
+DW = C + 32
+ZW = C + DW
+BIG = 2.0 ** 98
 UP, TINY = 1.25 * 2.0 ** -24, 2.0 ** -124
 Q4, U8 = "float8_e4m3fn_x4", "uint8"
 
@@ -27,24 +33,38 @@ SCRATCH = {
     "i1": ("sbuf", [128, C], "int32"), "i2": ("sbuf", [128, C], "int32"),
     "i3": ("sbuf", [128, K], "int32"), "i4": ("sbuf", [128, K], "int32"),
     "i5": ("sbuf", [128, 8], "int32"), "i6": ("sbuf", [128, 1], "int32"),
-    "uoff": ("sbuf", [128, 8], "uint16"),
-    "own": ("sbuf", [128, C], "bfloat16"), "oth": ("sbuf", [128, C], "bfloat16"),
+    "i7": ("sbuf", [128, 1], "int32"), "i8": ("sbuf", [128, 1], "int32"), "i9": ("sbuf", [128, 1], "int32"),
+    "uoff": ("sbuf", [128, 8], "uint16"), "goff": ("sbuf", [128, 2], "uint16"),
+    "own": ("sbuf", [128, C], "bfloat16"), "keep": ("sbuf", [128, C], "bfloat16"), "cut": ("sbuf", [128, TW], "bfloat16"),
+    "seg": ("sbuf", [128, ZW], "bfloat16"), "b16": ("sbuf", [128, H0], "bfloat16"), "base": ("sbuf", [128, H0], "bfloat16"),
     "j4": ("sbuf", [128, C], "float32"), "step": ("sbuf", [128, K], "float32"),
-    "c1": ("sbuf", [128, 1], "float32"), "col": ("sbuf", [128, 1], "float32"),
+    "c1": ("sbuf", [128, 1], "float32"), "c2": ("sbuf", [128, 1], "float32"), "c3": ("sbuf", [128, 1], "float32"),
+    "cq": ("sbuf", [128, 1], "float32"), "col": ("sbuf", [128, 1], "float32"),
     "rm": ("sbuf", [128, C], "float32"), "hold": ("sbuf", [128, C], "float32"),
-    "eq": ("sbuf", [128, C], "bfloat16"), "tie": ("sbuf", [128, C], "bfloat16"),
-    "cmp": ("sbuf", [128, NV * C], "bfloat16"), "cnt": ("sbuf", [128, NV * (C // 2)], "float16"),
-    "sgn": ("sbuf", [128, NS * ROW], "bfloat16"),
-    "ab": ("sbuf", [128, NS], "float32"), "sup": ("sbuf", [128, NS], "float32"), "acc": ("sbuf", [128, NS], "float32"),
+    "eq": ("sbuf", [128, TW], "bfloat16"), "tie": ("sbuf", [128, C], "bfloat16"),
+    "m1": ("sbuf", [128, TB * C], "bfloat16"),
+    "m2": ("sbuf", [128, TB * H0], "bfloat16"),
+    "m3": ("sbuf", [128, TB * ROW], "bfloat16"),
+    "cnt": ("sbuf", [128, TB * HALF], "float16"),
+    "p1": ("sbuf", [128, HB * (TW + 1)], "float16"),
+    "p2": ("sbuf", [128, TB * (TW + 1)], "float16"), "p3": ("sbuf", [128, TB * (TW + 1)], "float16"),
+    "dd": ("sbuf", [128, DW], "bfloat16"),
+    "tt": ("sbuf", [128, ZW], "bfloat16"), "zs": ("sbuf", [128, ZW + 128], "bfloat16"),
+    "ab": ("sbuf", [128, NS3], "float32"), "sup": ("sbuf", [128, NS3], "float32"),
+    "acc": ("sbuf", [128, 2 * TB * HW], "float32"),
+    "a2": ("sbuf", [128, 32], "float32"), "rb": ("sbuf", [128, 32], "float32"),
     "roff": ("sbuf", [128, NB], "uint16"), "order": ("sbuf", [128, C], "float32"),
     "pick": ("sbuf", [128, K], "float32"), "off4": ("sbuf", [128, 4 * K // 16], "uint16"),
     "olt": ("sbuf", [128, K], "float32"), "yt": ("sbuf", [128, C], "float32"),
-    "ph": ("psum", [128, 512], "float32"), "pv": ("psum", [128, 512], "float32"), "ps": ("psum", [128, 512], "float32"),
+    "v2": ("psum", [128, 512], "float32"), "v3": ("psum", [128, 512], "float32"),
+    "pv": ("psum", [128, 512], "float32"), "ps": ("psum", [128, 512], "float32"),
     "pw": ("psum", [128, 4 * 512], "float32"),
 }
-SEMAPHORES = ["lx", "lx2", "lu", "la", "lw", "lv", "xc", "io1", "io2", "io3", "io4", "k1", "k2", "k3", "k4", "k5", "kown", "koth",
-              "qu", "gu", "qa", "qv", "qx", "qx2", "qp", "mmh", "mmv", "mms", "mmw", "rm1", "rm2", "h1", "h2", "eq", "tie",
-              "ab", "sup", "f3", "ca", "cb", "cc", "sc", "sd", "rof1", "roff", "order", "pick", "off4", "xs", "p1a", "p1b", "acc",
+SEMAPHORES = ["lx1", "lx2", "lx3", "lu", "la", "lw", "lv", "xc", "io1", "io2", "io3", "io4", "io5", "io6",
+              "k0", "k1", "k2", "k3", "k4", "k5", "k6", "k7", "k8", "k9", "kown", "keep", "qu", "gu", "qa", "qv",
+              "qx1", "qx2", "qx3", "qp", "mm1", "mm2", "mm3", "mmv", "mms", "mw0", "mw1", "mw2", "mw3",
+              "rm1", "rm2", "rm3", "h1", "h2", "h3", "dc", "tie", "ab", "sup", "ca", "cc", "sa", "sb", "s2", "s3", "sc", "se",
+              "pf1", "pf2", "pf3", "df", "tr", "zs", "a2", "rb", "roff", "order", "pick", "off4", "xs", "acc2", "acc3",
               "relu", "pg", "olt", "ya", "yb", "outa", "outb", "sent", "ar1", "ar2", "ar3", "hop1", "hop2", "hop3"]
 
 
@@ -119,10 +139,10 @@ def rank_program(g, core, T, topo):
     else:
         arrive = len(topo.engines(fa, core)) + len(topo.engines(fb, core))
 
-    inc(S.dma_start(T.xs[:, 4 * H0:4 * C], T.x[:, 4 * H0:4 * C]), "lx", 16)
     inc(SY.dma_start(T.ut[:], T.u[:]), "lu", 16)
-    inc(S.dma_start(T.xs[:, 0:4 * H0], T.x[:, 0:4 * H0]), "lx2", 16)
-    wait(SY, "lx2")
+    inc(S.dma_start(T.xs[:, 4 * TW:4 * C], T.x[:, 4 * TW:4 * C]), "lx2", 16)
+    inc(SY.dma_start(T.xs[:, 0:4 * TW], T.x[:, 0:4 * TW]), "lx1", 16)
+    wait(SY, "lx1", "lx2")
     inc(SY.dma_start(T.pt[:, 4 * PAD:4 * (PAD + K)], T.a[:]), "la", 16)
     inc(SY.dma_start(T.wp[:], T.ws[:]), "lw", 16)
     inc(SY.dma_start(T.wq[:].bitcast(dt.uint8), T.wc[:]), "lw", 16)
@@ -131,158 +151,227 @@ def rank_program(g, core, T, topo):
 
     inc(g.iota(T.i5[:], [[16, 8]], 0, 0), "io1")
     inc(g.iota(T.i1[:], [[0, NB], [-1, 16]], 16, 1), "io3")
+    inc(g.iota(T.i7[:], [[0, 1]], 0, 17), "io5")
+    inc(g.iota(T.b16[:], [[16, H0 // 16], [0, 16]], 0, 0, allow_small_or_imprecise_dtypes=True), "io6")
     inc(g.iota(T.i3[:], [[0, K // 4], [-4, 4]], 16, 1), "io2")
     inc(g.iota(T.j4[:], [[4, C]], 0, 0, allow_small_or_imprecise_dtypes=True), "io4")
+    inc(V.memset(T.cut[:], BIG), "k0")
+    inc(V.memset(T.seg[:], 1.0), "k0")
+    inc(V.memset(T.dd[:], 0.0), "k0")
     inc(V.memset(T.pt[:, 0:4 * PAD], 0.0), "k1")
     wait(V, "io1")
     inc(V.tensor_copy(T.uoff[:], T.i5[:]), "k1")
     wait(V, "io3")
     inc(V.tensor_scalar(T.i2[:], T.i1[:], 15, None, Alu.bitwise_and), "k4")
-    wait(V, "io2")
-    inc(V.tensor_scalar(T.i4[:], T.i3[:], 12, None, Alu.bitwise_and), "k2")
-    inc(V.tensor_scalar(T.i6[:], T.i3[:, 0:1], 3, None, Alu.bitwise_and), "k2")
+    wait(V, "k0")
+    inc(V.memset(T.cut[:, 0:TW:16], -BIG), "k9")
+    inc(V.memset(T.seg[:, 0:ZW:16], 0.0), "k9")
+    wait(V, "io5")
+    inc(V.tensor_scalar(T.i8[:], T.i7[:], 16, None, Alu.bitwise_and), "k6")
+    inc(V.tensor_scalar(T.i9[:], T.i7[:], 15, None, Alu.bitwise_and), "k6")
     wait(V, "k4")
-    inc(V.tensor_scalar(T.own[:], T.i2[:], 0.0, None, Alu.is_equal), "kown")
+    inc(V.tensor_scalar(T.own[:], T.i2[:], 0.0, 0.5, Alu.is_equal, Alu.subtract), "kown")
     wait(S, "kown")
-    inc(S.activation(T.oth[:], T.own[:], Act.Identity, bias=1.0, scale=-1.0), "koth")
+    inc(S.activation(T.keep[:], T.own[:], Act.Identity, scale=2.0 * BIG), "keep")
+    inc(V.memset(T.m1[:, 0:TB * TW], 0.0), "k9")
 
     wait(V, "lu")
     inc(V.quantize_mx(T.uq[:], T.up[:], T.ut[:]), "qu")
-    wait(V, "k2")
-    inc(V.tensor_scalar(T.step[:], T.i4[:], 0.0, -1.0e6, Alu.is_equal, Alu.mult), "k3")
-    inc(V.tensor_scalar(T.c1[:], T.i4[:, 0:1], 512.0, -6144.0, Alu.mult, Alu.add), "k3")
+    wait(V, "k6")
+    inc(V.tensor_copy(T.cq[:], T.i9[:]), "k7")
+    inc(V.tensor_scalar(T.c2[:], T.i8[:], (C + 16) / 16.0, 15.0, Alu.mult, Alu.add), "k7")
+    inc(V.tensor_scalar(T.c3[:], T.i8[:], (C + 16) / 16.0, 271.0, Alu.mult, Alu.add), "k7")
     wait(V, "k1", "qu")
     inc(V.tensor_copy(T.gq[:].bitcast(dt.uint32), T.uq[:].bitcast(dt.uint32).indirect(T.uoff[:])), "gu")
     inc(V.tensor_copy(T.gp[:], T.up[:].indirect(T.uoff[:])), "gu")
     wait(PE, "gu")
 
-    half = C // 2
-    NH = C - H0
+    piece = {1: T.pw, 2: T.v2, 3: T.v3}
+
+    def cols(i):
+        return TW * (i - 1), TW * i
+
     for t in range(R):
         last = t == R - 1
-        wait(V, "lx" if t == 0 else "xs")
-        inc(V.quantize_mx(T.xq[:, H0:C], T.xp[:, H0:C], T.xs[:, 4 * H0:4 * C]), "qx")
-        if t == 0:
-            wait(V, "lx2")
-        inc(V.quantize_mx(T.xq[:, 0:H0], T.xp[:, 0:H0], T.xs[:, 0:4 * H0]), "qx2")
         lo = K * t
-        if t == 0:
-            wait(V, "k3")
-            inc(V.tensor_scalar(T.step[:], T.step[:], 2048.0, None, Alu.add), "k5")
-            inc(V.tensor_tensor(T.col[:], T.c1[:], T.i6[:], Alu.add), "k5")
-        else:
-            wait(V, "pg")
-            o = 128 * (t - 1)
-            inc(V.quantize_mx(T.pq[:, o:o + 128], T.pp[:, o:o + 128], T.pt[:, 4 * lo:4 * lo + 512]), "qp")
-            wait(g, "qp")
-            h = K * (t - 1)
-            da, db = landing(T, t) if direct else (T.hq[:, h:h + K].bitcast(dt.uint8), T.hp[:, h:h + K])
-            sem = T.sem[("ar%d" if direct else "hop%d") % t]
-            rid, pid = topo.addr(to_a, core)
-            g.remote_dma(da, T.pq[:, o + PAD:o + 128].bitcast(dt.uint8), sem, T.sem.sent, pid, rid, mask_of(ea))
-            rid, pid = topo.addr(to_b, core)
-            g.remote_dma(db, T.pp[:, o + PAD:o + 128], sem, T.sem.sent, pid, rid, mask_of(eb))
-
-        wait(PE, "qx")
-        inc(PE.matmul_mx(T.ph[:, 0:NH], T.gq[:], T.gp[:], T.xq[:, H0:C], T.xp[:, H0:C], True, True), "mmh")
-        wait(PE, "qx2")
+        if t > 0:
+            wait(V, "xs")
+        for i in (2, 3, 1):
+            a, b = cols(i)
+            if t == 0 and i != 3:
+                wait(V, "lx%d" % i)
+            inc(V.quantize_mx(T.xq[:, a:b], T.xp[:, a:b], T.xs[:, 4 * a:4 * b]), "qx%d" % i)
+            wait(PE, "qx%d" % i)
+            inc(PE.matmul_mx(piece[i][:, 0:TW], T.gq[:], T.gp[:], T.xq[:, a:b], T.xp[:, a:b], True, True), "mm%d" % i)
+        inc(PE.matmul_mx(T.ps[:, 0:H0], T.gq[:], T.gp[:], T.xq[:, TW:C], T.xp[:, TW:C], True, True), "mms")
         inc(PE.matmul_mx(T.pv[:, 0:C], T.gq[:], T.gp[:], T.xq[:], T.xp[:], True, True), "mmv")
-        inc(PE.matmul_mx(T.ps[:, 0:C], T.gq[:], T.gp[:], T.xq[:], T.xp[:], True, True), "mms")
 
-        wait(V, "mmh")
         if t == 0:
-            wait(V, "kown", "koth")
-        inc(V.tensor_tensor(T.rm[:, H0:C], T.ph[:, 0:NH], T.own[:, H0:C], Alu.mult), "rm1")
-        wait(V, "mmv")
-        inc(V.tensor_tensor(T.rm[:, 0:H0], T.pv[:, 0:H0], T.own[:, 0:H0], Alu.mult), "rm2")
-        wait(V, "rm1")
-        inc(V.tensor_tensor_scan(T.hold[:, H0:C], T.oth[:, H0:C], T.rm[:, H0:C], 0.0, Alu.mult, Alu.add), "h1")
-        wait(V, "rm2")
-        inc(V.tensor_tensor_scan(T.hold[:, 0:H0], T.oth[:, 0:H0], T.rm[:, 0:H0], 0.0, Alu.mult, Alu.add), "h2")
-        wait(V, "h1")
-        inc(V.tensor_tensor(T.eq[:, H0:C], T.pv[:, H0:C], T.hold[:, H0:C], Alu.is_equal), "eq")
+            inc(V.memset(T.m2[:, 0:TB * TW], 0.0), "k9")
+            wait(V, "keep", "k9")
+        for i in (2, 3, 1):
+            a, b = cols(i)
+            wait(V, "mm%d" % i)
+            inc(V.tensor_tensor(T.rm[:, a:b], piece[i][:, 0:TW], T.keep[:, a:b], Alu.min), "rm%d" % i)
+        for i in (2, 3, 1):
+            a, b = cols(i)
+            wait(V, "rm%d" % i)
+            inc(V.tensor_tensor_scan(T.hold[:, a:b], T.cut[:], T.rm[:, a:b], -BIG, Alu.min, Alu.max), "h%d" % i)
         wait(V, "h2")
-        inc(V.tensor_tensor(T.eq[:, 0:H0], T.pv[:, 0:H0], T.hold[:, 0:H0], Alu.is_equal), "eq")
+        inc(V.tensor_tensor(T.m2[:, TB - 1:TB * TW:TB], T.v2[:, 0:TW], T.hold[:, TW:H0], Alu.is_lt), "dc")
+        wait(V, "h3")
+        inc(V.tensor_tensor(T.eq[:], T.v3[:, 0:TW], T.hold[:, H0:C], Alu.is_equal), "dc")
+        wait(V, "h1")
+        inc(V.tensor_tensor(T.m1[:, TB - 1:TB * TW:TB], T.pw[:, 0:TW], T.hold[:, 0:TW], Alu.is_lt), "dc")
 
-        wait(S, "h1")
-        inc(S.activation(T.ab[:], T.hold[:, H0 + 15:C:16], Act.Abs, bias=TINY, scale=UP), "ab")
-        wait(S, "mms")
-        for i in range(NS - 1):
-            e = 16 * (NV + i) + 16
-            inc(S.activation(T.sgn[:, ROW * i + e:ROW * i + C], T.ps[:, e:C], Act.Sign, bias=T.hold[:, e - 1:e], scale=-1.0), "p1a")
-        wait(V, "ab")
-        inc(V.tensor_tensor(T.sup[:], T.hold[:, H0 + 15:C:16], T.ab[:], Alu.add), "sup")
-        wait(S, "sup")
-        for i in range(NS):
-            e = 16 * (NV + i) + 16
-            inc(S.activation(T.sgn[:, ROW * i:ROW * i + e], T.ps[:, 0:e], Act.Sign, bias=T.sup[:, i:i + 1], scale=-1.0),
-                "p1a" if i < NS - 1 else "p1b")
+        def signs2(k, name):
+            e = 16 * k + 16
+            inc(S.activation(T.m2[:, TB * e + k:TB * H0:TB], T.ps[:, e:H0], Act.Sign,
+                             bias=T.hold[:, TW + e - 1:TW + e], scale=-1.0), name)
 
-        def compare(c, name):
+        wait(S, "h2", "mms")
+        signs2(0, "sa")
+        wait(S, "h3")
+        inc(S.activation(T.ab[:], T.hold[:, H0 + 15:H0 + 16 * NS3:16], Act.Abs, bias=TINY, scale=UP), "ab")
+        for k in range(1, TB):
+            signs2(k, "sa" if k < TB - 2 else "sb")
+        wait(S, "sa")
+        for k in range(TB):
+            if k == TB - 2:
+                wait(S, "sb")
+            v = T.m2[:, TB * (16 * k + 16) + k:TB * H0:TB]
+            inc(S.activation(v, v, Act.Relu, accum_out=T.acc[:, HW * k + HW - 1:HW * k + HW]), "acc2")
+
+        wait(V, "mmv")
+        for c in range(TB):
             e = 16 * c + 16
-            s = T.hold[:, e - 1:e]
-            inc(V.tensor_scalar(T.cmp[:, C * c:C * c + e], T.pv[:, 0:e], s, None, Alu.is_le), name)
-            inc(V.tensor_scalar(T.cmp[:, C * c + e:C * c + C], T.pv[:, e:C], s, None, Alu.is_lt), name)
-
-        def add_up(c, name):
-            inc(V.tensor_tensor_scan(T.cnt[:, half * c:half * c + half], T.cmp[:, C * c:C * c + half], T.cmp[:, C * c + half:C * c + C],
-                                     T.tie[:, 16 * c + 15:16 * c + 16], Alu.add, Alu.add), name)
-
-        for c in range(N1):
-            compare(c, "ca")
+            inc(V.tensor_scalar(T.m1[:, TB * e + c:TB * C:TB], T.pv[:, e:C], T.hold[:, e - 1:e], None, Alu.is_lt), "ca")
             if c == 0:
-                wait(V, "eq")
-                inc(V.tensor_tensor_scan(T.tie[:], T.oth[:], T.eq[:], 0.0, Alu.mult, Alu.subtract), "tie")
+                if t == 0:
+                    wait(V, "k7", "io6")
+                    inc(V.tensor_scalar(T.base[:], T.b16[:], T.cq[:], None, Alu.add), "k3")
+                wait(V, "dc")
+                inc(V.tensor_tensor_scan(T.tie[:, H0:C], T.seg[:, 0:TW], T.eq[:], 0.0, Alu.mult, Alu.subtract), "tie")
+                wait(V, "ab")
+                inc(V.tensor_tensor(T.sup[:], T.hold[:, H0 + 15:H0 + 16 * NS3:16], T.ab[:], Alu.add), "sup")
             if c == 1:
-                wait(V, "tie")
-                inc(V.tensor_scalar(T.sgn[:, C:ROW * NS:ROW], T.tie[:, H0 + 15:C:16], 16.0, None, Alu.add), "f3")
-            if c == 6 and t == 0:
+                if t == 0:
+                    wait(V, "k3")
+                inc(V.tensor_tensor_scan(T.tie[:, 0:TW], T.base[:, 0:TW], T.m1[:, TB - 1:TB * TW:TB], 0.0, Alu.max, Alu.add), "tie")
+                inc(V.tensor_tensor_scan(T.tie[:, TW:H0], T.base[:, TW:H0], T.m2[:, TB - 1:TB * TW:TB], 0.0, Alu.max, Alu.add), "tie")
+            if t == 0 and c == 2:
+                inc(V.tensor_scalar(T.goff[:, 0:1], T.i9[:], 16.0, T.c2[:], Alu.mult, Alu.add), "k8")
+                inc(V.tensor_scalar(T.goff[:, 1:2], T.i9[:], 16.0, T.c3[:], Alu.mult, Alu.add), "k8")
+                inc(V.memset(T.zs[:, ZW:ZW + 128], 0.0), "k8")
+                inc(V.memset(T.a2[:, NB:32], 0.0), "k8")
+                inc(V.memset(T.m3[:, TW:TB * ROW:ROW], float(H0)), "k8")
+                inc(V.tensor_copy(T.p1[:, 0:HB], T.dd[:, 0:HB]), "k8")
+                inc(V.tensor_copy(T.p2[:, 0:TB], T.dd[:, 0:TB]), "k8")
+                inc(V.tensor_copy(T.p3[:, 0:TB], T.dd[:, 0:TB]), "k8")
+            if t == 0 and c == 3:
                 wait(V, "la")
                 inc(V.quantize_mx(T.lq[:, 0:128], T.lp[:, 0:128], T.pt[:, 0:512]), "qa")
+                wait(V, "io2")
+                inc(V.tensor_scalar(T.i4[:], T.i3[:], 12, None, Alu.bitwise_and), "k2")
+                inc(V.tensor_scalar(T.i6[:], T.i3[:, 0:1], 3, None, Alu.bitwise_and), "k2")
+            if t == 0 and c == 4:
+                wait(V, "k2")
+                inc(V.tensor_scalar(T.step[:], T.i4[:], 0.0, -1.0e6, Alu.is_equal, Alu.mult), "k3")
+                inc(V.tensor_scalar(T.c1[:], T.i4[:, 0:1], 512.0, -6144.0, Alu.mult, Alu.add), "k3")
+            if t == 0 and c == 5:
+                wait(V, "k3")
+                inc(V.tensor_scalar(T.step[:], T.step[:], 2048.0, None, Alu.add), "k5")
+                inc(V.tensor_tensor(T.col[:], T.c1[:], T.i6[:], Alu.add), "k5")
 
-        wait(S, "f3", "p1a")
-        for i in range(NS):
-            if i == NS - 1:
-                wait(S, "p1b")
-            v = T.sgn[:, ROW * i:ROW * i + C + 1]
-            inc(S.activation(v, v, Act.Relu, accum_out=T.acc[:, i:i + 1]), "acc")
+        wait(S, "sup")
+        for k in range(NS3):
+            e = 16 * k + 16
+            name = "s2" if k < NS3 - 1 else "s3"
+            inc(S.activation(T.m3[:, ROW * k:ROW * k + e], T.ps[:, TW:TW + e], Act.Sign, bias=T.sup[:, k:k + 1], scale=-1.0), name)
+            if e < TW:
+                inc(S.activation(T.m3[:, ROW * k + e:ROW * k + TW], T.ps[:, TW + e:H0], Act.Sign,
+                                 bias=T.hold[:, H0 + e - 1:H0 + e], scale=-1.0), name)
+        wait(S, "s2")
+        if t == 0:
+            wait(S, "k8")
+        for k in range(NS3):
+            if k == NS3 - 1:
+                wait(S, "s3")
+            v = T.m3[:, ROW * k:ROW * k + TW + 1]
+            inc(S.activation(v, v, Act.Relu, accum_out=T.acc[:, HW * (TB + k) + HW - 1:HW * (TB + k) + HW]), "acc3")
 
+        wait(PE, "dc")
         if t == 0:
             wait(PE, "qa", "lw")
         else:
             PE.wait_ge(T.sem["ar%d" % t], arrive)
         for b in range(4):
             inc(PE.matmul_mx(T.pw[:, 512 * b:512 * b + 128], T.wq[:, 128 * b:128 * b + 128], T.wp[:, 128 * b:128 * b + 128],
-                             T.lq[:, lo:lo + 128], T.lp[:, lo:lo + 128], True, True), "mmw")
-        wait(S, "mmw")
+                             T.lq[:, lo:lo + 128], T.lp[:, lo:lo + 128], True, True), "mw%d" % b)
         for b in range(4):
+            wait(S, "mw%d" % b)
             inc(S.activation(T.et[:, b:4 * K:4], T.pw[:, 512 * b + PAD:512 * b + 128], Act.Relu, scale=0.03125), "relu")
 
-        compare(N1, "cb")
-        wait(V, "ca")
-        for c in range(N1):
-            add_up(c, "sc")
-        compare(N1 + 1, "cc")
+        def add_up(*cs):
+            for c in cs:
+                e = 16 * c + 16
+                w = (C - e) // 2
+                inc(V.tensor_tensor_scan(T.cnt[:, HALF * (c + 1) - w:HALF * (c + 1)], T.m1[:, TB * e + c:TB * (e + w):TB],
+                                         T.m1[:, TB * (e + w) + c:TB * C:TB], T.tie[:, e - 1:e], Alu.add, Alu.add), "sc")
+
+        def differ(i, p, w):
+            wait(V, "pf%d" % i)
+            inc(V.tensor_tensor_scan(T.dd[:, 16 + TW * (i - 1):16 + TW * i], p[:, 2 * w - 1:w * (TW + 1):w], p[:, w - 1:w * TW:w],
+                                     0.0, Alu.max, Alu.subtract), "df")
+
+        for k in range(NS3, TB):
+            e = 16 * k + 16
+            s = T.hold[:, H0 + e - 1:H0 + e]
+            inc(V.tensor_scalar(T.m3[:, ROW * k:ROW * k + e], T.v3[:, 0:e], s, None, Alu.is_le), "cc")
+            if e < TW:
+                inc(V.tensor_scalar(T.m3[:, ROW * k + e:ROW * k + TW], T.v3[:, e:TW], s, None, Alu.is_lt), "cc")
+        wait(V, "ca", "tie")
+        if t == 0:
+            wait(V, "k8")
+        inc(V.tensor_tensor_scan(T.p1[:, HB:HB * (TW + 1)], T.m1[:, 0:TB * TW:2], T.m1[:, 1:TB * TW:2], 0.0, Alu.add, Alu.add), "pf1")
+        wait(V, "acc2")
+        inc(V.tensor_tensor_scan(T.p2[:, TB:TB * (TW + 1)], T.m1[:, TB * TW:TB * H0], T.m2[:, 0:TB * TW], 0.0, Alu.add, Alu.add), "pf2")
+        inc(V.tensor_tensor_scan(T.p3[:, TB:TB * (TW + 1)], T.m1[:, TB * H0:TB * C], T.m2[:, TB * TW:TB * H0],
+                                 0.0, Alu.add, Alu.add), "pf3")
+        differ(1, T.p1, HB)
+        differ(2, T.p2, TB)
+        if NS3 < TB:
+            wait(V, "cc")
+        for k in range(NS3, TB):
+            inc(V.tensor_tensor_scan(T.acc[:, HW * (TB + k):HW * (TB + k + 1)], T.m3[:, ROW * k:ROW * k + HW],
+                                     T.m3[:, ROW * k + HW:ROW * k + TW], float(H0), Alu.add, Alu.add), "se")
+        add_up(0)
+        differ(3, T.p3, TB)
+        add_up(1, 2, 3)
+        wait(V, "df")
+        inc(V.transpose(T.tt[:, 0:C], T.dd[:, 16:16 + C]), "tr")
+        inc(V.transpose(T.tt[:, C:ZW], T.dd[:]), "tr")
+        add_up(4, 5, 6, 7)
+        wait(V, "tr")
+        inc(V.tensor_tensor_scan(T.zs[:, 0:ZW], T.seg[:], T.tt[:], 0.0, Alu.mult, Alu.add), "zs")
         wait(V, "sc")
-        inc(V.tensor_copy(T.roff[:, 0:N1], T.cnt[:, half - 1:half * N1:half]), "rof1")
-        wait(V, "cb")
-        add_up(N1, "sd")
-        wait(V, "cc")
-        add_up(N1 + 1, "sd")
-        wait(V, "rof1")
+        inc(V.tensor_copy(T.a2[:, 0:TB], T.cnt[:, HALF - 1:HALF * TB:HALF]), "a2")
+        wait(V, "acc3")
+        if NS3 < TB:
+            wait(V, "se")
+        inc(V.tensor_tensor(T.a2[:, TB:NB], T.acc[:, HW - 1:2 * TB * HW:HW], T.tie[:, TW + 15:C:16], Alu.add), "a2")
+        wait(V, "zs", "a2")
+        inc(V.tensor_tensor(T.rb[:], T.zs[:].indirect(T.goff[:]), T.a2[:], Alu.subtract), "rb")
+        wait(V, "rb")
+        inc(V.tensor_scalar(T.roff[:], T.rb[:, 0:NB], -1.0, None, Alu.mult), "roff")
+        wait(V, "roff")
         if t == 0:
             wait(V, "io4", "k5")
-        inc(V.tensor_copy(T.order[:].indirect(T.roff[:, 0:N1]), T.j4[:, 0:16 * N1]), "order")
-        wait(V, "acc")
-        inc(V.tensor_scalar(T.roff[:, NV:NB], T.acc[:], -16.0, None, Alu.add), "roff")
-        wait(V, "sd")
-        inc(V.tensor_copy(T.roff[:, N1:NV], T.cnt[:, half * N1 + half - 1:half * NV:half]), "roff")
-        wait(V, "roff", "order")
-        inc(V.tensor_copy(T.order[:].indirect(T.roff[:, N1:NB]), T.j4[:, 16 * N1:C]), "order")
+        inc(V.tensor_copy(T.order[:].indirect(T.roff[:]), T.j4[:]), "order")
 
         wait(V, "order")
         inc(V.tensor_tensor_scan(T.pick[:], T.step[:], T.order[:, 0:K], 0.0, Alu.add, Alu.max), "pick")
-        if t == 1:
+        if t == 0:
             wait(V, "lv")
             inc(V.quantize_mx(T.vq[:], T.vp[:], T.vt[:]), "qv")
         wait(V, "pick")
@@ -299,6 +388,17 @@ def rank_program(g, core, T, topo):
             if t < R - 2:
                 wait(SY, "xs", "pg")
                 inc(SY.dma_start(T.xc[:], T.xs[:]), "xc", 16)
+            wait(V, "pg")
+            o = 128 * t
+            inc(V.quantize_mx(T.pq[:, o:o + 128], T.pp[:, o:o + 128], T.pt[:, p0 - 4 * PAD:p0 + 4 * K]), "qp")
+            wait(g, "qp")
+            h = K * t
+            da, db = landing(T, t + 1) if direct else (T.hq[:, h:h + K].bitcast(dt.uint8), T.hp[:, h:h + K])
+            sem = T.sem[("ar%d" if direct else "hop%d") % (t + 1)]
+            rid, pid = topo.addr(to_a, core)
+            g.remote_dma(da, T.pq[:, o + PAD:o + 128].bitcast(dt.uint8), sem, T.sem.sent, pid, rid, mask_of(ea))
+            rid, pid = topo.addr(to_b, core)
+            g.remote_dma(db, T.pp[:, o + PAD:o + 128], sem, T.sem.sent, pid, rid, mask_of(eb))
         else:
             wait(S, "order")
             inc(S.activation(T.olt[:], T.order[:, 0:K], Act.Identity, scale=0.25), "olt")
@@ -306,26 +406,26 @@ def rank_program(g, core, T, topo):
             inc(SY.dma_start(T.ol[:], T.olt[0:128:16, :]), "outa", 16)
 
     wait(V, "xs")
-    inc(V.quantize_mx(T.xq[:, 0:half], T.xp[:, 0:half], T.xs[:, 0:4 * half]), "qx")
-    inc(V.quantize_mx(T.xq[:, half:C], T.xp[:, half:C], T.xs[:, 4 * half:4 * C]), "qx2")
-    wait(PE, "qv", "qx")
-    inc(PE.matmul_mx(T.ps[:, 0:half], T.vq[:], T.vp[:], T.xq[:, 0:half], T.xp[:, 0:half], True, True), "mms")
+    inc(V.quantize_mx(T.xq[:, 0:HALF], T.xp[:, 0:HALF], T.xs[:, 0:4 * HALF]), "qx1")
+    inc(V.quantize_mx(T.xq[:, HALF:C], T.xp[:, HALF:C], T.xs[:, 4 * HALF:4 * C]), "qx2")
+    wait(PE, "qv", "qx1")
+    inc(PE.matmul_mx(T.ps[:, 0:HALF], T.vq[:], T.vp[:], T.xq[:, 0:HALF], T.xp[:, 0:HALF], True, True), "mms")
     wait(PE, "qx2")
-    inc(PE.matmul_mx(T.pv[:, 0:half], T.vq[:], T.vp[:], T.xq[:, half:C], T.xp[:, half:C], True, True), "mmv")
+    inc(PE.matmul_mx(T.pv[:, 0:HALF], T.vq[:], T.vp[:], T.xq[:, HALF:C], T.xp[:, HALF:C], True, True), "mmv")
     wait(S, "mms")
-    inc(S.activation(T.yt[:, 0:half], T.ps[:, 0:half], Act.Copy), "ya")
+    inc(S.activation(T.yt[:, 0:HALF], T.ps[:, 0:HALF], Act.Copy), "ya")
     wait(V, "mmv")
-    inc(V.tensor_copy(T.yt[:, half:C], T.pv[:, 0:half]), "yb")
-    wait(SY, "qx", "qx2")
+    inc(V.tensor_copy(T.yt[:, HALF:C], T.pv[:, 0:HALF]), "yb")
+    wait(SY, "qx1", "qx2")
     inc(SY.dma_start(T.oc[:], T.xq[:].bitcast(dt.uint8)), "outa", 16)
     for k in range(2):
         inc(SY.dma_start(T.osc[4 * k:4 * k + 4, :], T.xp[32 * k:32 * k + 4, :]), "outa", 16)
     wait(S, "ya", "qx2")
-    inc(S.dma_start(T.y[:, 0:half], T.yt[:, 0:half]), "outb", 16)
+    inc(S.dma_start(T.y[:, 0:HALF], T.yt[:, 0:HALF]), "outb", 16)
     for k in range(2, 4):
         inc(S.dma_start(T.osc[4 * k:4 * k + 4, :], T.xp[32 * k:32 * k + 4, :]), "outb", 16)
     wait(SY, "yb")
-    inc(SY.dma_start(T.y[:, half:C], T.yt[:, half:C]), "outa", 16)
+    inc(SY.dma_start(T.y[:, HALF:C], T.yt[:, HALF:C]), "outa", 16)
     wait(SY, "outa")
     wait(S, "outb")
     g.wait_ge(T.sem.sent, (R - 1) * (len(ea) + len(eb)))

@@ -30,12 +30,12 @@ SCRATCH = {
     "hq": ("sbuf", [128, K * (R - 1)], Q4), "hp": ("sbuf", [128, K * (R - 1)], U8),
     "lq": ("sbuf", [128, PAD + R * K], Q4), "lp": ("sbuf", [128, PAD + R * K], U8),
     "et": ("sbuf", [128, 4 * K], "bfloat16"),
-    "i1": ("sbuf", [128, C], "int32"), "i2": ("sbuf", [128, C], "int32"),
+    "i1": ("sbuf", [128, TW], "int32"), "i2": ("sbuf", [128, TW], "int32"),
     "i3": ("sbuf", [128, K], "int32"), "i4": ("sbuf", [128, K], "int32"),
     "i5": ("sbuf", [128, 8], "int32"), "i6": ("sbuf", [128, 1], "int32"),
     "i7": ("sbuf", [128, 1], "int32"), "i8": ("sbuf", [128, 1], "int32"), "i9": ("sbuf", [128, 1], "int32"),
     "uoff": ("sbuf", [128, 8], "uint16"), "goff": ("sbuf", [128, 2], "uint16"),
-    "own": ("sbuf", [128, C], "bfloat16"), "keep": ("sbuf", [128, C], "bfloat16"), "cut": ("sbuf", [128, TW], "bfloat16"),
+    "own": ("sbuf", [128, TW], "bfloat16"), "keep": ("sbuf", [128, TW], "bfloat16"), "cut": ("sbuf", [128, TW], "bfloat16"),
     "seg": ("sbuf", [128, ZW], "bfloat16"), "b16": ("sbuf", [128, H0], "bfloat16"), "base": ("sbuf", [128, H0], "bfloat16"),
     "j4": ("sbuf", [128, C], "float32"), "step": ("sbuf", [128, K], "float32"),
     "c1": ("sbuf", [128, 1], "float32"), "c2": ("sbuf", [128, 1], "float32"), "c3": ("sbuf", [128, 1], "float32"),
@@ -45,14 +45,14 @@ SCRATCH = {
     "m1": ("sbuf", [128, TB * C], "bfloat16"),
     "m2": ("sbuf", [128, TB * H0], "bfloat16"),
     "m3": ("sbuf", [128, TB * ROW], "bfloat16"),
-    "cnt": ("sbuf", [128, TB * HALF], "float16"),
+    "cnt": ("sbuf", [128, 32 * HALF], "float16"),
     "p1": ("sbuf", [128, HB * (TW + 1)], "float16"),
     "p2": ("sbuf", [128, TB * (TW + 1)], "float16"), "p3": ("sbuf", [128, TB * (TW + 1)], "float16"),
     "dd": ("sbuf", [128, DW], "bfloat16"),
     "tt": ("sbuf", [128, ZW], "bfloat16"), "zs": ("sbuf", [128, ZW + 128], "bfloat16"),
     "ab": ("sbuf", [128, NS3], "float32"), "sup": ("sbuf", [128, NS3], "float32"),
     "acc": ("sbuf", [128, 2 * TB * HW], "float32"),
-    "a2": ("sbuf", [128, 32], "float32"), "rb": ("sbuf", [128, 32], "float32"),
+    "rb": ("sbuf", [128, 32], "float32"),
     "roff": ("sbuf", [128, NB], "uint16"), "order": ("sbuf", [128, C], "float32"),
     "pick": ("sbuf", [128, K], "float32"), "off4": ("sbuf", [128, 4 * K // 16], "uint16"),
     "olt": ("sbuf", [128, K], "float32"), "yt": ("sbuf", [128, C], "float32"),
@@ -61,7 +61,7 @@ SCRATCH = {
     "pw": ("psum", [128, 4 * 512], "float32"),
 }
 SEMAPHORES = ["lx1", "lx2", "lx3", "lu", "la", "lw", "lv", "xc", "io1", "io2", "io3", "io4", "io5", "io6",
-              "k0", "k1", "k2", "k3", "k4", "k5", "k6", "k7", "k8", "k9", "kown", "keep", "qu", "gu", "qa", "qv",
+              "k0", "k1", "k2", "k3", "k4", "k5", "k6", "k7", "k8", "k9", "kz", "kown", "keep", "qu", "gu", "qa", "qv",
               "qx1", "qx2", "qx3", "qp", "mm1", "mm2", "mm3", "mmv", "mms", "mw0", "mw1", "mw2", "mw3",
               "rm1", "rm2", "rm3", "h1", "h2", "h3", "dc", "tie", "ab", "sup", "ca", "cc", "sa", "sb", "s2", "s3", "sc", "se",
               "pf1", "pf2", "pf3", "df", "tr", "zs", "a2", "rb", "roff", "order", "pick", "off4", "xs", "acc2", "acc3",
@@ -139,10 +139,14 @@ def rank_program(g, core, T, topo):
     else:
         arrive = len(topo.engines(fa, core)) + len(topo.engines(fb, core))
 
+    def cols(i):
+        return TW * (i - 1), TW * i
+
     inc(SY.dma_start(T.ut[:], T.u[:]), "lu", 16)
-    inc(S.dma_start(T.xs[:, 4 * TW:4 * C], T.x[:, 4 * TW:4 * C]), "lx2", 16)
-    inc(SY.dma_start(T.xs[:, 0:4 * TW], T.x[:, 0:4 * TW]), "lx1", 16)
-    wait(SY, "lx1", "lx2")
+    for q, i in ((S, 2), (SY, 3), (S, 1)):
+        a, b = cols(i)
+        inc(q.dma_start(T.xs[:, 4 * a:4 * b], T.x[:, 4 * a:4 * b]), "lx%d" % i, 16)
+    wait(SY, "lx1", "lx2", "lx3")
     inc(SY.dma_start(T.pt[:, 4 * PAD:4 * (PAD + K)], T.a[:]), "la", 16)
     inc(SY.dma_start(T.wp[:], T.ws[:]), "lw", 16)
     inc(SY.dma_start(T.wq[:].bitcast(dt.uint8), T.wc[:]), "lw", 16)
@@ -150,74 +154,91 @@ def rank_program(g, core, T, topo):
     inc(SY.dma_start(T.vt[:], T.v[:]), "lv", 16)
 
     inc(g.iota(T.i5[:], [[16, 8]], 0, 0), "io1")
-    inc(g.iota(T.i1[:], [[0, NB], [-1, 16]], 16, 1), "io3")
     inc(g.iota(T.i7[:], [[0, 1]], 0, 17), "io5")
+    inc(g.iota(T.i1[:], [[0, TB], [-1, 16]], 16, 1), "io3")
     inc(g.iota(T.b16[:], [[16, H0 // 16], [0, 16]], 0, 0, allow_small_or_imprecise_dtypes=True), "io6")
     inc(g.iota(T.i3[:], [[0, K // 4], [-4, 4]], 16, 1), "io2")
     inc(g.iota(T.j4[:], [[4, C]], 0, 0, allow_small_or_imprecise_dtypes=True), "io4")
-    inc(V.memset(T.cut[:], BIG), "k0")
     inc(V.memset(T.seg[:], 1.0), "k0")
+    inc(V.memset(T.cut[:], BIG), "k0")
     inc(V.memset(T.dd[:], 0.0), "k0")
-    inc(V.memset(T.pt[:, 0:4 * PAD], 0.0), "k1")
-    wait(V, "io1")
-    inc(V.tensor_copy(T.uoff[:], T.i5[:]), "k1")
-    wait(V, "io3")
+    wait(V, "io1", "io5", "io3")
     inc(V.tensor_scalar(T.i2[:], T.i1[:], 15, None, Alu.bitwise_and), "k4")
+    inc(V.tensor_scalar(T.i8[:], T.i7[:], 16, None, Alu.bitwise_and), "k4")
+    inc(V.tensor_scalar(T.i9[:], T.i7[:], 15, None, Alu.bitwise_and), "k4")
     wait(V, "k0")
-    inc(V.memset(T.cut[:, 0:TW:16], -BIG), "k9")
     inc(V.memset(T.seg[:, 0:ZW:16], 0.0), "k9")
-    wait(V, "io5")
-    inc(V.tensor_scalar(T.i8[:], T.i7[:], 16, None, Alu.bitwise_and), "k6")
-    inc(V.tensor_scalar(T.i9[:], T.i7[:], 15, None, Alu.bitwise_and), "k6")
+    inc(V.memset(T.cut[:, 0:TW:16], -BIG), "k9")
+    inc(V.tensor_copy(T.uoff[:], T.i5[:]), "k1")
+    inc(V.memset(T.pt[:, 0:4 * PAD], 0.0), "k1")
     wait(V, "k4")
     inc(V.tensor_scalar(T.own[:], T.i2[:], 0.0, 0.5, Alu.is_equal, Alu.subtract), "kown")
-    wait(S, "kown")
-    inc(S.activation(T.keep[:], T.own[:], Act.Identity, scale=2.0 * BIG), "keep")
-    inc(V.memset(T.m1[:, 0:TB * TW], 0.0), "k9")
-
-    wait(V, "lu")
-    inc(V.quantize_mx(T.uq[:], T.up[:], T.ut[:]), "qu")
-    wait(V, "k6")
     inc(V.tensor_copy(T.cq[:], T.i9[:]), "k7")
     inc(V.tensor_scalar(T.c2[:], T.i8[:], (C + 16) / 16.0, 15.0, Alu.mult, Alu.add), "k7")
     inc(V.tensor_scalar(T.c3[:], T.i8[:], (C + 16) / 16.0, 271.0, Alu.mult, Alu.add), "k7")
-    wait(V, "k1", "qu")
-    inc(V.tensor_copy(T.gq[:].bitcast(dt.uint32), T.uq[:].bitcast(dt.uint32).indirect(T.uoff[:])), "gu")
-    inc(V.tensor_copy(T.gp[:], T.up[:].indirect(T.uoff[:])), "gu")
-    wait(PE, "gu")
+    inc(V.tensor_copy(T.p1[:, 0:HB], T.dd[:, 0:HB]), "k8")
+    inc(V.tensor_copy(T.p2[:, 0:TB], T.dd[:, 0:TB]), "k8")
+    inc(V.tensor_copy(T.p3[:, 0:TB], T.dd[:, 0:TB]), "k8")
+    inc(V.tensor_copy(T.cnt[:, HALF * (NB + 1) - 1:32 * HALF:HALF], T.dd[:, 0:32 - NB]), "k8")
+    inc(V.memset(T.zs[:, ZW:ZW + 128], 0.0), "k8")
+    inc(V.memset(T.m3[:, TW:TB * ROW:ROW], float(H0)), "k8")
+    wait(V, "k7")
+    inc(V.tensor_scalar(T.goff[:, 0:1], T.i9[:], 16.0, T.c2[:], Alu.mult, Alu.add), "k8")
+    inc(V.tensor_scalar(T.goff[:, 1:2], T.i9[:], 16.0, T.c3[:], Alu.mult, Alu.add), "k8")
+    wait(S, "kown")
+    inc(S.activation(T.keep[:], T.own[:], Act.Identity, scale=2.0 * BIG), "keep")
+    wait(S, "k9")
+    for m in (T.m2, T.m1):
+        for a in (0, 512):
+            inc(S.activation(m[:, a:a + 512], T.seg[:, 0:512], Act.Identity, scale=0.0), "kz")
+    wait(S, "k7", "io6")
+    inc(S.activation(T.base[:], T.b16[:], Act.Identity, bias=T.cq[:]), "kz")
 
     piece = {1: T.pw, 2: T.v2, 3: T.v3}
 
-    def cols(i):
-        return TW * (i - 1), TW * i
+    def quantise(i):
+        a, b = cols(i)
+        inc(V.quantize_mx(T.xq[:, a:b], T.xp[:, a:b], T.xs[:, 4 * a:4 * b]), "qx%d" % i)
 
     for t in range(R):
         last = t == R - 1
         lo = K * t
-        if t > 0:
+        if t == 0:
+            wait(V, "lu")
+            inc(V.quantize_mx(T.uq[:], T.up[:], T.ut[:]), "qu")
+            wait(V, "lx2")
+            quantise(2)
+            wait(V, "k1", "qu")
+            inc(V.tensor_copy(T.gq[:].bitcast(dt.uint32), T.uq[:].bitcast(dt.uint32).indirect(T.uoff[:])), "gu")
+            inc(V.tensor_copy(T.gp[:], T.up[:].indirect(T.uoff[:])), "gu")
+            wait(PE, "gu")
+            wait(V, "lx3")
+            quantise(3)
+            wait(V, "lx1")
+            quantise(1)
+            wait(V, "keep", "k9")
+        else:
             wait(V, "xs")
+            for i in (2, 3, 1):
+                quantise(i)
         for i in (2, 3, 1):
             a, b = cols(i)
-            if t == 0 and i != 3:
-                wait(V, "lx%d" % i)
-            inc(V.quantize_mx(T.xq[:, a:b], T.xp[:, a:b], T.xs[:, 4 * a:4 * b]), "qx%d" % i)
             wait(PE, "qx%d" % i)
             inc(PE.matmul_mx(piece[i][:, 0:TW], T.gq[:], T.gp[:], T.xq[:, a:b], T.xp[:, a:b], True, True), "mm%d" % i)
         inc(PE.matmul_mx(T.ps[:, 0:H0], T.gq[:], T.gp[:], T.xq[:, TW:C], T.xp[:, TW:C], True, True), "mms")
         inc(PE.matmul_mx(T.pv[:, 0:C], T.gq[:], T.gp[:], T.xq[:], T.xp[:], True, True), "mmv")
 
-        if t == 0:
-            inc(V.memset(T.m2[:, 0:TB * TW], 0.0), "k9")
-            wait(V, "keep", "k9")
         for i in (2, 3, 1):
             a, b = cols(i)
             wait(V, "mm%d" % i)
-            inc(V.tensor_tensor(T.rm[:, a:b], piece[i][:, 0:TW], T.keep[:, a:b], Alu.min), "rm%d" % i)
+            inc(V.tensor_tensor(T.rm[:, a:b], piece[i][:, 0:TW], T.keep[:], Alu.min), "rm%d" % i)
         for i in (2, 3, 1):
             a, b = cols(i)
             wait(V, "rm%d" % i)
             inc(V.tensor_tensor_scan(T.hold[:, a:b], T.cut[:], T.rm[:, a:b], -BIG, Alu.min, Alu.max), "h%d" % i)
         wait(V, "h2")
+        if t == 0:
+            wait(V, "kz")
         inc(V.tensor_tensor(T.m2[:, TB - 1:TB * TW:TB], T.v2[:, 0:TW], T.hold[:, TW:H0], Alu.is_lt), "dc")
         wait(V, "h3")
         inc(V.tensor_tensor(T.eq[:], T.v3[:, 0:TW], T.hold[:, H0:C], Alu.is_equal), "dc")
@@ -229,6 +250,8 @@ def rank_program(g, core, T, topo):
             inc(S.activation(T.m2[:, TB * e + k:TB * H0:TB], T.ps[:, e:H0], Act.Sign,
                              bias=T.hold[:, TW + e - 1:TW + e], scale=-1.0), name)
 
+        if t == 0:
+            wait(S, "kz")
         wait(S, "h2", "mms")
         signs2(0, "sa")
         wait(S, "h3")
@@ -242,51 +265,35 @@ def rank_program(g, core, T, topo):
             v = T.m2[:, TB * (16 * k + 16) + k:TB * H0:TB]
             inc(S.activation(v, v, Act.Relu, accum_out=T.acc[:, HW * k + HW - 1:HW * k + HW]), "acc2")
 
+        def compare3(k):
+            e = 16 * k + 16
+            s = T.hold[:, H0 + e - 1:H0 + e]
+            inc(V.tensor_scalar(T.m3[:, ROW * k:ROW * k + e], T.v3[:, 0:e], s, None, Alu.is_le), "cc")
+            if e < TW:
+                inc(V.tensor_scalar(T.m3[:, ROW * k + e:ROW * k + TW], T.v3[:, e:TW], s, None, Alu.is_lt), "cc")
+
         wait(V, "mmv")
         for c in range(TB):
             e = 16 * c + 16
             inc(V.tensor_scalar(T.m1[:, TB * e + c:TB * C:TB], T.pv[:, e:C], T.hold[:, e - 1:e], None, Alu.is_lt), "ca")
             if c == 0:
-                if t == 0:
-                    wait(V, "k7", "io6")
-                    inc(V.tensor_scalar(T.base[:], T.b16[:], T.cq[:], None, Alu.add), "k3")
                 wait(V, "dc")
                 inc(V.tensor_tensor_scan(T.tie[:, H0:C], T.seg[:, 0:TW], T.eq[:], 0.0, Alu.mult, Alu.subtract), "tie")
+                inc(V.tensor_tensor_scan(T.tie[:, 0:TW], T.base[:, 0:TW], T.m1[:, TB - 1:TB * TW:TB], 0.0, Alu.max, Alu.add), "tie")
+            if c == 1:
                 wait(V, "ab")
                 inc(V.tensor_tensor(T.sup[:], T.hold[:, H0 + 15:H0 + 16 * NS3:16], T.ab[:], Alu.add), "sup")
-            if c == 1:
-                if t == 0:
-                    wait(V, "k3")
-                inc(V.tensor_tensor_scan(T.tie[:, 0:TW], T.base[:, 0:TW], T.m1[:, TB - 1:TB * TW:TB], 0.0, Alu.max, Alu.add), "tie")
-                inc(V.tensor_tensor_scan(T.tie[:, TW:H0], T.base[:, TW:H0], T.m2[:, TB - 1:TB * TW:TB], 0.0, Alu.max, Alu.add), "tie")
-            if t == 0 and c == 2:
-                inc(V.tensor_scalar(T.goff[:, 0:1], T.i9[:], 16.0, T.c2[:], Alu.mult, Alu.add), "k8")
-                inc(V.tensor_scalar(T.goff[:, 1:2], T.i9[:], 16.0, T.c3[:], Alu.mult, Alu.add), "k8")
-                inc(V.memset(T.zs[:, ZW:ZW + 128], 0.0), "k8")
-                inc(V.memset(T.a2[:, NB:32], 0.0), "k8")
-                inc(V.memset(T.m3[:, TW:TB * ROW:ROW], float(H0)), "k8")
-                inc(V.tensor_copy(T.p1[:, 0:HB], T.dd[:, 0:HB]), "k8")
-                inc(V.tensor_copy(T.p2[:, 0:TB], T.dd[:, 0:TB]), "k8")
-                inc(V.tensor_copy(T.p3[:, 0:TB], T.dd[:, 0:TB]), "k8")
-            if t == 0 and c == 3:
+            if t == 0 and c == 5:
                 wait(V, "la")
                 inc(V.quantize_mx(T.lq[:, 0:128], T.lp[:, 0:128], T.pt[:, 0:512]), "qa")
-                wait(V, "io2")
-                inc(V.tensor_scalar(T.i4[:], T.i3[:], 12, None, Alu.bitwise_and), "k2")
-                inc(V.tensor_scalar(T.i6[:], T.i3[:, 0:1], 3, None, Alu.bitwise_and), "k2")
-            if t == 0 and c == 4:
-                wait(V, "k2")
-                inc(V.tensor_scalar(T.step[:], T.i4[:], 0.0, -1.0e6, Alu.is_equal, Alu.mult), "k3")
-                inc(V.tensor_scalar(T.c1[:], T.i4[:, 0:1], 512.0, -6144.0, Alu.mult, Alu.add), "k3")
-            if t == 0 and c == 5:
-                wait(V, "k3")
-                inc(V.tensor_scalar(T.step[:], T.step[:], 2048.0, None, Alu.add), "k5")
-                inc(V.tensor_tensor(T.col[:], T.c1[:], T.i6[:], Alu.add), "k5")
+        for k in range(NS3, TB):
+            compare3(k)
+        inc(V.tensor_tensor_scan(T.tie[:, TW:H0], T.base[:, TW:H0], T.m2[:, TB - 1:TB * TW:TB], 0.0, Alu.max, Alu.add), "k6")
 
         wait(S, "sup")
         for k in range(NS3):
             e = 16 * k + 16
-            name = "s2" if k < NS3 - 1 else "s3"
+            name = "s2" if k < NS3 - 2 else "s3"
             inc(S.activation(T.m3[:, ROW * k:ROW * k + e], T.ps[:, TW:TW + e], Act.Sign, bias=T.sup[:, k:k + 1], scale=-1.0), name)
             if e < TW:
                 inc(S.activation(T.m3[:, ROW * k + e:ROW * k + TW], T.ps[:, TW + e:H0], Act.Sign,
@@ -295,7 +302,7 @@ def rank_program(g, core, T, topo):
         if t == 0:
             wait(S, "k8")
         for k in range(NS3):
-            if k == NS3 - 1:
+            if k == NS3 - 2:
                 wait(S, "s3")
             v = T.m3[:, ROW * k:ROW * k + TW + 1]
             inc(S.activation(v, v, Act.Relu, accum_out=T.acc[:, HW * (TB + k) + HW - 1:HW * (TB + k) + HW]), "acc3")
@@ -324,12 +331,6 @@ def rank_program(g, core, T, topo):
             inc(V.tensor_tensor_scan(T.dd[:, 16 + TW * (i - 1):16 + TW * i], p[:, 2 * w - 1:w * (TW + 1):w], p[:, w - 1:w * TW:w],
                                      0.0, Alu.max, Alu.subtract), "df")
 
-        for k in range(NS3, TB):
-            e = 16 * k + 16
-            s = T.hold[:, H0 + e - 1:H0 + e]
-            inc(V.tensor_scalar(T.m3[:, ROW * k:ROW * k + e], T.v3[:, 0:e], s, None, Alu.is_le), "cc")
-            if e < TW:
-                inc(V.tensor_scalar(T.m3[:, ROW * k + e:ROW * k + TW], T.v3[:, e:TW], s, None, Alu.is_lt), "cc")
         wait(V, "ca", "tie")
         if t == 0:
             wait(V, "k8")
@@ -353,27 +354,38 @@ def rank_program(g, core, T, topo):
         inc(V.transpose(T.tt[:, C:ZW], T.dd[:]), "tr")
         add_up(4, 5, 6, 7)
         wait(V, "tr")
-        inc(V.tensor_tensor_scan(T.zs[:, 0:ZW], T.seg[:], T.tt[:], 0.0, Alu.mult, Alu.add), "zs")
-        wait(V, "sc")
-        inc(V.tensor_copy(T.a2[:, 0:TB], T.cnt[:, HALF - 1:HALF * TB:HALF]), "a2")
-        wait(V, "acc3")
+        inc(V.tensor_tensor_scan(T.zs[:, 0:ZW], T.seg[:], T.tt[:], 0.0, Alu.mult, Alu.subtract), "zs")
+        wait(V, "acc3", "k6")
         if NS3 < TB:
             wait(V, "se")
-        inc(V.tensor_tensor(T.a2[:, TB:NB], T.acc[:, HW - 1:2 * TB * HW:HW], T.tie[:, TW + 15:C:16], Alu.add), "a2")
-        wait(V, "zs", "a2")
-        inc(V.tensor_tensor(T.rb[:], T.zs[:].indirect(T.goff[:]), T.a2[:], Alu.subtract), "rb")
-        wait(V, "rb")
-        inc(V.tensor_scalar(T.roff[:], T.rb[:, 0:NB], -1.0, None, Alu.mult), "roff")
-        wait(V, "roff")
+        inc(V.tensor_tensor(T.cnt[:, HALF * (TB + 1) - 1:HALF * NB:HALF], T.acc[:, HW - 1:2 * TB * HW:HW], T.tie[:, TW + 15:C:16],
+                            Alu.add), "a2")
         if t == 0:
-            wait(V, "io4", "k5")
+            wait(V, "io2")
+            inc(V.tensor_scalar(T.i4[:], T.i3[:], 12, None, Alu.bitwise_and), "k2")
+            inc(V.tensor_scalar(T.i6[:], T.i3[:, 0:1], 3, None, Alu.bitwise_and), "k2")
+        wait(V, "zs", "a2", "sc")
+        inc(V.tensor_tensor(T.rb[:], T.zs[:].indirect(T.goff[:]), T.cnt[:, HALF - 1:32 * HALF:HALF], Alu.add), "rb")
+        if t == 0:
+            wait(V, "k2")
+            inc(V.tensor_scalar(T.step[:], T.i4[:], 0.0, -1.0e6, Alu.is_equal, Alu.mult), "k3")
+            inc(V.tensor_scalar(T.c1[:], T.i4[:, 0:1], 512.0, -6144.0, Alu.mult, Alu.add), "k3")
+        wait(V, "rb")
+        inc(V.tensor_copy(T.roff[:], T.rb[:, 0:NB]), "roff")
+        if t == 0:
+            wait(V, "k3")
+            inc(V.tensor_scalar(T.step[:], T.step[:], 2048.0, None, Alu.add), "k5")
+            inc(V.tensor_tensor(T.col[:], T.c1[:], T.i6[:], Alu.add), "k5")
+            wait(V, "io4")
+        wait(V, "roff")
         inc(V.tensor_copy(T.order[:].indirect(T.roff[:]), T.j4[:]), "order")
 
-        wait(V, "order")
-        inc(V.tensor_tensor_scan(T.pick[:], T.step[:], T.order[:, 0:K], 0.0, Alu.add, Alu.max), "pick")
         if t == 0:
             wait(V, "lv")
             inc(V.quantize_mx(T.vq[:], T.vp[:], T.vt[:]), "qv")
+            wait(V, "k5")
+        wait(V, "order")
+        inc(V.tensor_tensor_scan(T.pick[:], T.step[:], T.order[:, 0:K], 0.0, Alu.add, Alu.max), "pick")
         wait(V, "pick")
         inc(V.tensor_scalar(T.off4[:], T.pick[:, 3:K:4], T.col[:], None, Alu.add), "off4")
         wait(V, "off4", "relu")
@@ -385,9 +397,6 @@ def rank_program(g, core, T, topo):
             wait(S, "off4", "xc")
             p0 = 4 * (PAD + K * (t + 1))
             inc(S.activation(T.pt[:, p0:p0 + 4 * K], T.xc[:].indirect(T.off4[:]), Act.Copy), "pg")
-            if t < R - 2:
-                wait(SY, "xs", "pg")
-                inc(SY.dma_start(T.xc[:], T.xs[:]), "xc", 16)
             wait(V, "pg")
             o = 128 * t
             inc(V.quantize_mx(T.pq[:, o:o + 128], T.pp[:, o:o + 128], T.pt[:, p0 - 4 * PAD:p0 + 4 * K]), "qp")
@@ -399,6 +408,10 @@ def rank_program(g, core, T, topo):
             g.remote_dma(da, T.pq[:, o + PAD:o + 128].bitcast(dt.uint8), sem, T.sem.sent, pid, rid, mask_of(ea))
             rid, pid = topo.addr(to_b, core)
             g.remote_dma(db, T.pp[:, o + PAD:o + 128], sem, T.sem.sent, pid, rid, mask_of(eb))
+            if t < R - 2:
+                wait(SY, "xs", "pg")
+                SY.wait_ge(T.sem.sent, (t + 1) * (len(ea) + len(eb)))
+                inc(SY.dma_start(T.xc[:], T.xs[:]), "xc", 16)
         else:
             wait(S, "order")
             inc(S.activation(T.olt[:], T.order[:, 0:K], Act.Identity, scale=0.25), "olt")

from concourse.mybir import dt, AluOpType as Alu, ActivationFunctionType as Act

C, K, R = 384, 96, 4
NB = C // 16
TW = 128
TB = TW // 16
NS3 = 7
H0 = 2 * TW
HW = TW // 2
HB = TB // 2
HALF = C // 2
PAD = 128 - K
ROW = TW + 2
DW = C + 32
ZW = C + DW
BIG = 2.0 ** 98
UP, TINY = 1.25 * 2.0 ** -24, 2.0 ** -124
Q4, U8 = "float8_e4m3fn_x4", "uint8"

SCRATCH = {
    "xs": ("sbuf", [128, 4 * C], "bfloat16"),
    "xc": ("sbuf", [128, 4 * C], "bfloat16"),
    "xq": ("sbuf", [128, C], Q4), "xp": ("sbuf", [128, C], U8),
    "ut": ("sbuf", [128, 512], "bfloat16"), "uq": ("sbuf", [128, 128], Q4), "up": ("sbuf", [128, 128], U8),
    "gq": ("sbuf", [128, 128], Q4), "gp": ("sbuf", [128, 128], U8),
    "vt": ("sbuf", [128, 512], "bfloat16"), "vq": ("sbuf", [128, 128], Q4), "vp": ("sbuf", [128, 128], U8),
    "wq": ("sbuf", [128, 512], Q4), "wp": ("sbuf", [128, 512], U8),
    "pt": ("sbuf", [128, 4 * (PAD + R * K)], "bfloat16"),
    "pq": ("sbuf", [128, 128 * (R - 1)], Q4), "pp": ("sbuf", [128, 128 * (R - 1)], U8),
    "hq": ("sbuf", [128, K * (R - 1)], Q4), "hp": ("sbuf", [128, K * (R - 1)], U8),
    "lq": ("sbuf", [128, PAD + R * K], Q4), "lp": ("sbuf", [128, PAD + R * K], U8),
    "et": ("sbuf", [128, 4 * K], "bfloat16"),
    "i1": ("sbuf", [128, TW], "int32"), "i2": ("sbuf", [128, TW], "int32"),
    "i3": ("sbuf", [128, K], "int32"), "i4": ("sbuf", [128, K], "int32"),
    "i5": ("sbuf", [128, 8], "int32"), "i6": ("sbuf", [128, 1], "int32"),
    "i7": ("sbuf", [128, 1], "int32"), "i8": ("sbuf", [128, 1], "int32"), "i9": ("sbuf", [128, 1], "int32"),
    "uoff": ("sbuf", [128, 8], "uint16"), "goff": ("sbuf", [128, 2], "uint16"),
    "own": ("sbuf", [128, TW], "bfloat16"), "keep": ("sbuf", [128, TW], "bfloat16"), "cut": ("sbuf", [128, TW], "bfloat16"),
    "seg": ("sbuf", [128, ZW], "bfloat16"), "b16": ("sbuf", [128, H0], "bfloat16"), "base": ("sbuf", [128, H0], "bfloat16"),
    "j4": ("sbuf", [128, C], "float32"), "step": ("sbuf", [128, K], "float32"),
    "c1": ("sbuf", [128, 1], "float32"), "c2": ("sbuf", [128, 1], "float32"), "c3": ("sbuf", [128, 1], "float32"),
    "cq": ("sbuf", [128, 1], "float32"), "col": ("sbuf", [128, 1], "float32"),
    "rm": ("sbuf", [128, C], "float32"), "hold": ("sbuf", [128, C], "float32"),
    "eq": ("sbuf", [128, TW], "bfloat16"), "tie": ("sbuf", [128, C], "bfloat16"),
    "m1": ("sbuf", [128, TB * C], "bfloat16"),
    "m2": ("sbuf", [128, TB * H0], "bfloat16"),
    "m3": ("sbuf", [128, TB * ROW], "bfloat16"),
    "cnt": ("sbuf", [128, 32 * HALF], "float16"),
    "p1": ("sbuf", [128, HB * (TW + 1)], "float16"),
    "p2": ("sbuf", [128, TB * (TW + 1)], "float16"), "p3": ("sbuf", [128, TB * (TW + 1)], "float16"),
    "dd": ("sbuf", [128, DW], "bfloat16"),
    "tt": ("sbuf", [128, ZW], "bfloat16"), "zs": ("sbuf", [128, ZW + 128], "bfloat16"),
    "ab": ("sbuf", [128, NS3], "float32"), "sup": ("sbuf", [128, NS3], "float32"),
    "acc": ("sbuf", [128, 2 * TB * HW], "float32"),
    "rb": ("sbuf", [128, 32], "float32"),
    "roff": ("sbuf", [128, NB], "uint16"), "order": ("sbuf", [128, C], "float32"),
    "pick": ("sbuf", [128, K], "float32"), "off4": ("sbuf", [128, 4 * K // 16], "uint16"),
    "olt": ("sbuf", [128, K], "float32"), "yt": ("sbuf", [128, C], "float32"),
    "v2": ("psum", [128, 512], "float32"), "v3": ("psum", [128, 512], "float32"),
    "pv": ("psum", [128, 512], "float32"), "ps": ("psum", [128, 512], "float32"),
    "pw": ("psum", [128, 4 * 512], "float32"),
}
SEMAPHORES = ["lx1", "lx2", "lx3", "lu", "la", "lw", "lv", "xc", "io1", "io2", "io3", "io4", "io5", "io6",
              "k0", "k1", "k2", "k3", "k4", "k5", "k6", "k7", "k8", "k9", "kz", "kown", "keep", "qu", "gu", "qa", "qv",
              "qx1", "qx2", "qx3", "qp", "mm1", "mm2", "mm3", "mmv", "mms", "mw0", "mw1", "mw2", "mw3",
              "rm1", "rm2", "rm3", "h1", "h2", "h3", "dc", "tie", "ab", "sup", "ca", "cc", "sa", "sb", "s2", "s3", "sc", "se",
              "pf1", "pf2", "pf3", "df", "tr", "zs", "a2", "rb", "roff", "order", "pick", "off4", "xs", "acc2", "acc3",
              "relu", "pg", "olt", "ya", "yb", "outa", "outb", "sent", "ar1", "ar2", "ar3", "hop1", "hop2", "hop3"]


def mask_of(engines):
    m = 0
    for e in engines:
        m |= 1 << e
    return m


def way(T, topo, r):
    src, dst = T.cores[r], T.cores[(r + 1) % len(T.cores)]
    if topo.may_write(src, dst):
        return dst, dst
    via = [c for c in topo.cores_of(src) if T.rank_of(c) is None and topo.die(c) == topo.die(src) and topo.may_write(c, dst)]
    return via[0], via[1]


def first_leg(topo, src, a, b):
    return topo.engines(src, a)[:8], topo.engines(src, b)[-4:]


def landing(T, t):
    lo = PAD + K * t
    return T.lq[:, lo:lo + K].bitcast(dt.uint8), T.lp[:, lo:lo + K]


def hand_on(g, core, T, topo):
    n = len(T.cores)
    for r in range(n):
        a, b = way(T, topo, r)
        if core not in (a, b):
            continue
        src, dst = T.cores[r], T.cores[(r + 1) % n]
        ea, eb = first_leg(topo, src, a, b)
        out = topo.engines(core, dst)
        rid, pid = topo.addr(dst, core)
        for t in range(1, R):
            lo = K * (t - 1)
            g.wait_ge(T.sem["hop%d" % t], len(ea) if core == a else len(eb))
            held = T.hq[:, lo:lo + K].bitcast(dt.uint8) if core == a else T.hp[:, lo:lo + K]
            g.remote_dma(landing(T, t)[0 if core == a else 1], held, T.sem["ar%d" % t], T.sem.sent, pid, rid, mask_of(out))
        g.wait_ge(T.sem.sent, (R - 1) * len(out))


def rank_program(g, core, T, topo):
    rank = T.rank_of(core)
    if rank is None:
        hand_on(g, core, T, topo)
        return
    n = len(T.cores)
    V, S, PE, SY = g.vector, g.scalar, g.tensor, g.sync
    count = {}

    def inc(ins, name, by=1):
        ins.then_inc(T.sem[name], by)
        count[name] = count.get(name, 0) + by

    def wait(q, *names):
        for name in names:
            q.wait_ge(T.sem[name], count[name])

    nxt = T.cores[(rank + 1) % n]
    to_a, to_b = way(T, topo, rank)
    ea, eb = first_leg(topo, core, to_a, to_b)
    direct = to_a == nxt
    prev = (rank - 1) % n
    fa, fb = way(T, topo, prev)
    if fa == core:
        pa, pb = first_leg(topo, T.cores[prev], fa, fb)
        arrive = len(pa) + len(pb)
    else:
        arrive = len(topo.engines(fa, core)) + len(topo.engines(fb, core))

    def cols(i):
        return TW * (i - 1), TW * i

    inc(SY.dma_start(T.ut[:], T.u[:]), "lu", 16)
    for q, i in ((S, 2), (SY, 3), (S, 1)):
        a, b = cols(i)
        inc(q.dma_start(T.xs[:, 4 * a:4 * b], T.x[:, 4 * a:4 * b]), "lx%d" % i, 16)
    wait(SY, "lx1", "lx2", "lx3")
    inc(SY.dma_start(T.pt[:, 4 * PAD:4 * (PAD + K)], T.a[:]), "la", 16)
    inc(SY.dma_start(T.wp[:], T.ws[:]), "lw", 16)
    inc(SY.dma_start(T.wq[:].bitcast(dt.uint8), T.wc[:]), "lw", 16)
    inc(SY.dma_start(T.xc[:], T.x[:]), "xc", 16)
    inc(SY.dma_start(T.vt[:], T.v[:]), "lv", 16)

    inc(g.iota(T.i5[:], [[16, 8]], 0, 0), "io1")
    inc(g.iota(T.i7[:], [[0, 1]], 0, 17), "io5")
    inc(g.iota(T.i1[:], [[0, TB], [-1, 16]], 16, 1), "io3")
    inc(g.iota(T.b16[:], [[16, H0 // 16], [0, 16]], 0, 0, allow_small_or_imprecise_dtypes=True), "io6")
    inc(g.iota(T.i3[:], [[0, K // 4], [-4, 4]], 16, 1), "io2")
    inc(g.iota(T.j4[:], [[4, C]], 0, 0, allow_small_or_imprecise_dtypes=True), "io4")
    inc(V.memset(T.seg[:], 1.0), "k0")
    inc(V.memset(T.cut[:], BIG), "k0")
    inc(V.memset(T.dd[:], 0.0), "k0")
    wait(V, "io1", "io5", "io3")
    inc(V.tensor_scalar(T.i2[:], T.i1[:], 15, None, Alu.bitwise_and), "k4")
    inc(V.tensor_scalar(T.i8[:], T.i7[:], 16, None, Alu.bitwise_and), "k4")
    inc(V.tensor_scalar(T.i9[:], T.i7[:], 15, None, Alu.bitwise_and), "k4")
    wait(V, "k0")
    inc(V.memset(T.seg[:, 0:ZW:16], 0.0), "k9")
    inc(V.memset(T.cut[:, 0:TW:16], -BIG), "k9")
    inc(V.tensor_copy(T.uoff[:], T.i5[:]), "k1")
    inc(V.memset(T.pt[:, 0:4 * PAD], 0.0), "k1")
    wait(V, "k4")
    inc(V.tensor_scalar(T.own[:], T.i2[:], 0.0, 0.5, Alu.is_equal, Alu.subtract), "kown")
    inc(V.tensor_copy(T.cq[:], T.i9[:]), "k7")
    inc(V.tensor_scalar(T.c2[:], T.i8[:], (C + 16) / 16.0, 15.0, Alu.mult, Alu.add), "k7")
    inc(V.tensor_scalar(T.c3[:], T.i8[:], (C + 16) / 16.0, 271.0, Alu.mult, Alu.add), "k7")
    inc(V.tensor_copy(T.p1[:, 0:HB], T.dd[:, 0:HB]), "k8")
    inc(V.tensor_copy(T.p2[:, 0:TB], T.dd[:, 0:TB]), "k8")
    inc(V.tensor_copy(T.p3[:, 0:TB], T.dd[:, 0:TB]), "k8")
    inc(V.tensor_copy(T.cnt[:, HALF * (NB + 1) - 1:32 * HALF:HALF], T.dd[:, 0:32 - NB]), "k8")
    inc(V.memset(T.zs[:, ZW:ZW + 128], 0.0), "k8")
    inc(V.memset(T.m3[:, TW:TB * ROW:ROW], float(H0)), "k8")
    wait(V, "k7")
    inc(V.tensor_scalar(T.goff[:, 0:1], T.i9[:], 16.0, T.c2[:], Alu.mult, Alu.add), "k8")
    inc(V.tensor_scalar(T.goff[:, 1:2], T.i9[:], 16.0, T.c3[:], Alu.mult, Alu.add), "k8")
    wait(S, "kown")
    inc(S.activation(T.keep[:], T.own[:], Act.Identity, scale=2.0 * BIG), "keep")
    wait(S, "k9")
    for m in (T.m2, T.m1):
        for a in (0, 512):
            inc(S.activation(m[:, a:a + 512], T.seg[:, 0:512], Act.Identity, scale=0.0), "kz")
    wait(S, "k7", "io6")
    inc(S.activation(T.base[:], T.b16[:], Act.Identity, bias=T.cq[:]), "kz")

    piece = {1: T.pw, 2: T.v2, 3: T.v3}

    def quantise(i):
        a, b = cols(i)
        inc(V.quantize_mx(T.xq[:, a:b], T.xp[:, a:b], T.xs[:, 4 * a:4 * b]), "qx%d" % i)

    for t in range(R):
        last = t == R - 1
        lo = K * t
        if t == 0:
            wait(V, "lu")
            inc(V.quantize_mx(T.uq[:], T.up[:], T.ut[:]), "qu")
            wait(V, "lx2")
            quantise(2)
            wait(V, "k1", "qu")
            inc(V.tensor_copy(T.gq[:].bitcast(dt.uint32), T.uq[:].bitcast(dt.uint32).indirect(T.uoff[:])), "gu")
            inc(V.tensor_copy(T.gp[:], T.up[:].indirect(T.uoff[:])), "gu")
            wait(PE, "gu")
            wait(V, "lx3")
            quantise(3)
            wait(V, "lx1")
            quantise(1)
            wait(V, "keep", "k9")
        else:
            wait(V, "xs")
            for i in (2, 3, 1):
                quantise(i)
        for i in (2, 3, 1):
            a, b = cols(i)
            wait(PE, "qx%d" % i)
            inc(PE.matmul_mx(piece[i][:, 0:TW], T.gq[:], T.gp[:], T.xq[:, a:b], T.xp[:, a:b], True, True), "mm%d" % i)
        inc(PE.matmul_mx(T.ps[:, 0:H0], T.gq[:], T.gp[:], T.xq[:, TW:C], T.xp[:, TW:C], True, True), "mms")
        inc(PE.matmul_mx(T.pv[:, 0:C], T.gq[:], T.gp[:], T.xq[:], T.xp[:], True, True), "mmv")

        for i in (2, 3, 1):
            a, b = cols(i)
            wait(V, "mm%d" % i)
            inc(V.tensor_tensor(T.rm[:, a:b], piece[i][:, 0:TW], T.keep[:], Alu.min), "rm%d" % i)
        for i in (2, 3, 1):
            a, b = cols(i)
            wait(V, "rm%d" % i)
            inc(V.tensor_tensor_scan(T.hold[:, a:b], T.cut[:], T.rm[:, a:b], -BIG, Alu.min, Alu.max), "h%d" % i)
        wait(V, "h2")
        if t == 0:
            wait(V, "kz")
        inc(V.tensor_tensor(T.m2[:, TB - 1:TB * TW:TB], T.v2[:, 0:TW], T.hold[:, TW:H0], Alu.is_lt), "dc")
        wait(V, "h3")
        inc(V.tensor_tensor(T.eq[:], T.v3[:, 0:TW], T.hold[:, H0:C], Alu.is_equal), "dc")
        wait(V, "h1")
        inc(V.tensor_tensor(T.m1[:, TB - 1:TB * TW:TB], T.pw[:, 0:TW], T.hold[:, 0:TW], Alu.is_lt), "dc")

        def signs2(k, name):
            e = 16 * k + 16
            inc(S.activation(T.m2[:, TB * e + k:TB * H0:TB], T.ps[:, e:H0], Act.Sign,
                             bias=T.hold[:, TW + e - 1:TW + e], scale=-1.0), name)

        if t == 0:
            wait(S, "kz")
        wait(S, "h2", "mms")
        signs2(0, "sa")
        wait(S, "h3")
        inc(S.activation(T.ab[:], T.hold[:, H0 + 15:H0 + 16 * NS3:16], Act.Abs, bias=TINY, scale=UP), "ab")
        for k in range(1, TB):
            signs2(k, "sa" if k < TB - 2 else "sb")
        wait(S, "sa")
        for k in range(TB):
            if k == TB - 2:
                wait(S, "sb")
            v = T.m2[:, TB * (16 * k + 16) + k:TB * H0:TB]
            inc(S.activation(v, v, Act.Relu, accum_out=T.acc[:, HW * k + HW - 1:HW * k + HW]), "acc2")

        def compare3(k):
            e = 16 * k + 16
            s = T.hold[:, H0 + e - 1:H0 + e]
            inc(V.tensor_scalar(T.m3[:, ROW * k:ROW * k + e], T.v3[:, 0:e], s, None, Alu.is_le), "cc")
            if e < TW:
                inc(V.tensor_scalar(T.m3[:, ROW * k + e:ROW * k + TW], T.v3[:, e:TW], s, None, Alu.is_lt), "cc")

        wait(V, "mmv")
        for c in range(TB):
            e = 16 * c + 16
            inc(V.tensor_scalar(T.m1[:, TB * e + c:TB * C:TB], T.pv[:, e:C], T.hold[:, e - 1:e], None, Alu.is_lt), "ca")
            if c == 0:
                wait(V, "dc")
                inc(V.tensor_tensor_scan(T.tie[:, H0:C], T.seg[:, 0:TW], T.eq[:], 0.0, Alu.mult, Alu.subtract), "tie")
                inc(V.tensor_tensor_scan(T.tie[:, 0:TW], T.base[:, 0:TW], T.m1[:, TB - 1:TB * TW:TB], 0.0, Alu.max, Alu.add), "tie")
            if c == 1:
                wait(V, "ab")
                inc(V.tensor_tensor(T.sup[:], T.hold[:, H0 + 15:H0 + 16 * NS3:16], T.ab[:], Alu.add), "sup")
            if t == 0 and c == 5:
                wait(V, "la")
                inc(V.quantize_mx(T.lq[:, 0:128], T.lp[:, 0:128], T.pt[:, 0:512]), "qa")
        for k in range(NS3, TB):
            compare3(k)
        inc(V.tensor_tensor_scan(T.tie[:, TW:H0], T.base[:, TW:H0], T.m2[:, TB - 1:TB * TW:TB], 0.0, Alu.max, Alu.add), "k6")

        wait(S, "sup")
        for k in range(NS3):
            e = 16 * k + 16
            name = "s2" if k < NS3 - 2 else "s3"
            inc(S.activation(T.m3[:, ROW * k:ROW * k + e], T.ps[:, TW:TW + e], Act.Sign, bias=T.sup[:, k:k + 1], scale=-1.0), name)
            if e < TW:
                inc(S.activation(T.m3[:, ROW * k + e:ROW * k + TW], T.ps[:, TW + e:H0], Act.Sign,
                                 bias=T.hold[:, H0 + e - 1:H0 + e], scale=-1.0), name)
        wait(S, "s2")
        if t == 0:
            wait(S, "k8")
        for k in range(NS3):
            if k == NS3 - 2:
                wait(S, "s3")
            v = T.m3[:, ROW * k:ROW * k + TW + 1]
            inc(S.activation(v, v, Act.Relu, accum_out=T.acc[:, HW * (TB + k) + HW - 1:HW * (TB + k) + HW]), "acc3")

        wait(PE, "dc")
        if t == 0:
            wait(PE, "qa", "lw")
        else:
            PE.wait_ge(T.sem["ar%d" % t], arrive)
        for b in range(4):
            inc(PE.matmul_mx(T.pw[:, 512 * b:512 * b + 128], T.wq[:, 128 * b:128 * b + 128], T.wp[:, 128 * b:128 * b + 128],
                             T.lq[:, lo:lo + 128], T.lp[:, lo:lo + 128], True, True), "mw%d" % b)
        for b in range(4):
            wait(S, "mw%d" % b)
            inc(S.activation(T.et[:, b:4 * K:4], T.pw[:, 512 * b + PAD:512 * b + 128], Act.Relu, scale=0.03125), "relu")

        def add_up(*cs):
            for c in cs:
                e = 16 * c + 16
                w = (C - e) // 2
                inc(V.tensor_tensor_scan(T.cnt[:, HALF * (c + 1) - w:HALF * (c + 1)], T.m1[:, TB * e + c:TB * (e + w):TB],
                                         T.m1[:, TB * (e + w) + c:TB * C:TB], T.tie[:, e - 1:e], Alu.add, Alu.add), "sc")

        def differ(i, p, w):
            wait(V, "pf%d" % i)
            inc(V.tensor_tensor_scan(T.dd[:, 16 + TW * (i - 1):16 + TW * i], p[:, 2 * w - 1:w * (TW + 1):w], p[:, w - 1:w * TW:w],
                                     0.0, Alu.max, Alu.subtract), "df")

        wait(V, "ca", "tie")
        if t == 0:
            wait(V, "k8")
        inc(V.tensor_tensor_scan(T.p1[:, HB:HB * (TW + 1)], T.m1[:, 0:TB * TW:2], T.m1[:, 1:TB * TW:2], 0.0, Alu.add, Alu.add), "pf1")
        wait(V, "acc2")
        inc(V.tensor_tensor_scan(T.p2[:, TB:TB * (TW + 1)], T.m1[:, TB * TW:TB * H0], T.m2[:, 0:TB * TW], 0.0, Alu.add, Alu.add), "pf2")
        inc(V.tensor_tensor_scan(T.p3[:, TB:TB * (TW + 1)], T.m1[:, TB * H0:TB * C], T.m2[:, TB * TW:TB * H0],
                                 0.0, Alu.add, Alu.add), "pf3")
        differ(1, T.p1, HB)
        differ(2, T.p2, TB)
        if NS3 < TB:
            wait(V, "cc")
        for k in range(NS3, TB):
            inc(V.tensor_tensor_scan(T.acc[:, HW * (TB + k):HW * (TB + k + 1)], T.m3[:, ROW * k:ROW * k + HW],
                                     T.m3[:, ROW * k + HW:ROW * k + TW], float(H0), Alu.add, Alu.add), "se")
        add_up(0)
        differ(3, T.p3, TB)
        add_up(1, 2, 3)
        wait(V, "df")
        inc(V.transpose(T.tt[:, 0:C], T.dd[:, 16:16 + C]), "tr")
        inc(V.transpose(T.tt[:, C:ZW], T.dd[:]), "tr")
        add_up(4, 5, 6, 7)
        wait(V, "tr")
        inc(V.tensor_tensor_scan(T.zs[:, 0:ZW], T.seg[:], T.tt[:], 0.0, Alu.mult, Alu.subtract), "zs")
        wait(V, "acc3", "k6")
        if NS3 < TB:
            wait(V, "se")
        inc(V.tensor_tensor(T.cnt[:, HALF * (TB + 1) - 1:HALF * NB:HALF], T.acc[:, HW - 1:2 * TB * HW:HW], T.tie[:, TW + 15:C:16],
                            Alu.add), "a2")
        if t == 0:
            wait(V, "io2")
            inc(V.tensor_scalar(T.i4[:], T.i3[:], 12, None, Alu.bitwise_and), "k2")
            inc(V.tensor_scalar(T.i6[:], T.i3[:, 0:1], 3, None, Alu.bitwise_and), "k2")
        wait(V, "zs", "a2", "sc")
        inc(V.tensor_tensor(T.rb[:], T.zs[:].indirect(T.goff[:]), T.cnt[:, HALF - 1:32 * HALF:HALF], Alu.add), "rb")
        if t == 0:
            wait(V, "k2")
            inc(V.tensor_scalar(T.step[:], T.i4[:], 0.0, -1.0e6, Alu.is_equal, Alu.mult), "k3")
            inc(V.tensor_scalar(T.c1[:], T.i4[:, 0:1], 512.0, -6144.0, Alu.mult, Alu.add), "k3")
        wait(V, "rb")
        inc(V.tensor_copy(T.roff[:], T.rb[:, 0:NB]), "roff")
        if t == 0:
            wait(V, "k3")
            inc(V.tensor_scalar(T.step[:], T.step[:], 2048.0, None, Alu.add), "k5")
            inc(V.tensor_tensor(T.col[:], T.c1[:], T.i6[:], Alu.add), "k5")
            wait(V, "io4")
        wait(V, "roff")
        inc(V.tensor_copy(T.order[:].indirect(T.roff[:]), T.j4[:]), "order")

        if t == 0:
            wait(V, "lv")
            inc(V.quantize_mx(T.vq[:], T.vp[:], T.vt[:]), "qv")
            wait(V, "k5")
        wait(V, "order")
        inc(V.tensor_tensor_scan(T.pick[:], T.step[:], T.order[:, 0:K], 0.0, Alu.add, Alu.max), "pick")
        wait(V, "pick")
        inc(V.tensor_scalar(T.off4[:], T.pick[:, 3:K:4], T.col[:], None, Alu.add), "off4")
        wait(V, "off4", "relu")
        if 0 < t < R - 1:
            wait(V, "xc")
        inc(V.tensor_copy(T.xs[:].indirect(T.off4[:]), T.et[:]), "xs")

        if not last:
            wait(S, "off4", "xc")
            p0 = 4 * (PAD + K * (t + 1))
            inc(S.activation(T.pt[:, p0:p0 + 4 * K], T.xc[:].indirect(T.off4[:]), Act.Copy), "pg")
            wait(V, "pg")
            o = 128 * t
            inc(V.quantize_mx(T.pq[:, o:o + 128], T.pp[:, o:o + 128], T.pt[:, p0 - 4 * PAD:p0 + 4 * K]), "qp")
            wait(g, "qp")
            h = K * t
            da, db = landing(T, t + 1) if direct else (T.hq[:, h:h + K].bitcast(dt.uint8), T.hp[:, h:h + K])
            sem = T.sem[("ar%d" if direct else "hop%d") % (t + 1)]
            rid, pid = topo.addr(to_a, core)
            g.remote_dma(da, T.pq[:, o + PAD:o + 128].bitcast(dt.uint8), sem, T.sem.sent, pid, rid, mask_of(ea))
            rid, pid = topo.addr(to_b, core)
            g.remote_dma(db, T.pp[:, o + PAD:o + 128], sem, T.sem.sent, pid, rid, mask_of(eb))
            if t < R - 2:
                wait(SY, "xs", "pg")
                SY.wait_ge(T.sem.sent, (t + 1) * (len(ea) + len(eb)))
                inc(SY.dma_start(T.xc[:], T.xs[:]), "xc", 16)
        else:
            wait(S, "order")
            inc(S.activation(T.olt[:], T.order[:, 0:K], Act.Identity, scale=0.25), "olt")
            wait(SY, "olt")
            inc(SY.dma_start(T.ol[:], T.olt[0:128:16, :]), "outa", 16)

    wait(V, "xs")
    inc(V.quantize_mx(T.xq[:, 0:HALF], T.xp[:, 0:HALF], T.xs[:, 0:4 * HALF]), "qx1")
    inc(V.quantize_mx(T.xq[:, HALF:C], T.xp[:, HALF:C], T.xs[:, 4 * HALF:4 * C]), "qx2")
    wait(PE, "qv", "qx1")
    inc(PE.matmul_mx(T.ps[:, 0:HALF], T.vq[:], T.vp[:], T.xq[:, 0:HALF], T.xp[:, 0:HALF], True, True), "mms")
    wait(PE, "qx2")
    inc(PE.matmul_mx(T.pv[:, 0:HALF], T.vq[:], T.vp[:], T.xq[:, HALF:C], T.xp[:, HALF:C], True, True), "mmv")
    wait(S, "mms")
    inc(S.activation(T.yt[:, 0:HALF], T.ps[:, 0:HALF], Act.Copy), "ya")
    wait(V, "mmv")
    inc(V.tensor_copy(T.yt[:, HALF:C], T.pv[:, 0:HALF]), "yb")
    wait(SY, "qx1", "qx2")
    inc(SY.dma_start(T.oc[:], T.xq[:].bitcast(dt.uint8)), "outa", 16)
    for k in range(2):
        inc(SY.dma_start(T.osc[4 * k:4 * k + 4, :], T.xp[32 * k:32 * k + 4, :]), "outa", 16)
    wait(S, "ya", "qx2")
    inc(S.dma_start(T.y[:, 0:HALF], T.yt[:, 0:HALF]), "outb", 16)
    for k in range(2, 4):
        inc(S.dma_start(T.osc[4 * k:4 * k + 4, :], T.xp[32 * k:32 * k + 4, :]), "outb", 16)
    wait(SY, "yb")
    inc(SY.dma_start(T.y[:, HALF:C], T.yt[:, HALF:C]), "outa", 16)
    wait(SY, "outa")
    wait(S, "outb")
    g.wait_ge(T.sem.sent, (R - 1) * (len(ea) + len(eb)))
